import numpy as np
import ml_dtypes


def mxq(x, axis, fmt="e4m3"):
    dtype, down = {"e4m3": (ml_dtypes.float8_e4m3fn, 7), "e5m2": (ml_dtypes.float8_e5m2, 14)}[fmt]
    v = np.moveaxis(np.asarray(x, np.float32).astype(ml_dtypes.bfloat16).astype(np.float64), axis, -1)
    blocks = v.reshape(v.shape[:-1] + (-1, 32))
    amax = np.abs(blocks).max(-1, keepdims=True)
    byte = np.maximum(np.where(amax > 0, np.frexp(amax)[1] - 1 + 127, 0) - down, 1)
    scale = np.exp2(byte - 127.0)
    codes = (blocks / scale).astype(np.float32).astype(dtype).astype(np.float64)
    return np.moveaxis((codes * scale).reshape(v.shape), -1, axis)


WIDE = False


def mx_kscale(k):
    if not WIDE:
        return np.ones(k)
    levels = np.array([10, -10, 5, -5, 0])
    if k % 512:
        return np.exp2(np.random.permutation(np.resize(levels, k // 32))).repeat(32)
    a = np.empty((k // 512, 16))
    for p in range(k // 512):
        a[p, :8] = np.random.permutation(np.resize(levels, 8))
        for g in range(8):
            far = levels[np.abs(levels - a[p, g]) >= 10]
            a[p, g + 8] = far[np.random.randint(len(far))]
    return np.exp2(a.ravel()).repeat(32)


def f64(x):
    return np.asarray(x).astype(np.float64)


def striped(idx):
    return np.tile(idx.reshape(-1, 16).T, (8, 1)).astype(np.uint16)


def unstriped(offs):
    return offs[:16].T.reshape(-1).astype(np.int64)


def silu(v):
    return v / (1.0 + np.exp(-np.maximum(v, -700.0)))


K, T, E, C, H, N = 1024, 512, 8, 128, 512, 256


def by_expert(wq, xq):
    return np.concatenate([wq[e].T @ xq[:, e * C:(e + 1) * C] for e in range(E)], axis=1)


def setup_inputs():
    n = np.random.standard_normal
    s = mx_kscale(K)[:, None]
    u = mx_kscale(H)
    first = np.random.permutation(np.repeat(np.arange(E), T // E))
    second = (first + 1 + np.random.permutation(np.repeat(np.arange(E - 1), -(-T // (E - 1)))[:T])) % E
    while np.bincount(second, minlength=E).max() != T // E:
        load = np.bincount(second, minlength=E); hi, lo = int(load.argmax()), int(load.argmin())
        t = np.flatnonzero((second == hi) & (first != lo))[0]; second[t] = lo
    slot_token = np.empty(E * C, np.int64); pos = np.empty((2, T), np.int64); fill = np.zeros(E, np.int64)
    place = np.stack([np.random.permutation(C) for _ in range(E)])
    for r, deal in enumerate((first, second)):
        for t in np.random.permutation(T):
            e = deal[t]; j = e * C + place[e, fill[e]]; fill[e] += 1; slot_token[j] = t; pos[r, t] = j
    g = np.random.uniform(0.2, 0.8, T)
    return {
        "xT": (n((K, T)) * s).astype(np.float32),
        "w1": (n((E, K, H)) / np.sqrt(K) / s[None] * u[None, None, :]).astype(np.float32),
        "w2": (n((E, H, N)) / np.sqrt(H) / u[None, :, None]).astype(np.float32),
        "gate": np.stack([np.tile(g, (N, 1)), np.tile(1.0 - g, (N, 1))]).astype(np.float32),
        "offs": striped(slot_token),
        "pos1": striped(pos[0]),
        "pos2": striped(pos[1]),
    }


def reference(xT, w1, w2, gate, offs, pos1, pos2):
    idx = unstriped(offs)
    xq = mxq(f64(xT)[:, idx], 0, "e4m3")
    h = silu(by_expert(mxq(f64(w1), 1, "e4m3"), xq))
    y = by_expert(mxq(f64(w2), 1, "e4m3"), mxq(h, 0, "e4m3"))
    return f64(gate[0]) * y[:, unstriped(pos1)] + f64(gate[1]) * y[:, unstriped(pos2)]

@@ -1,0 +1,219 @@
+from contextlib import ExitStack
+
+import concourse.mybir as mybir
+
+K, T, E, C, H, N = 1024, 512, 8, 128, 512, 256
+FLOPS = 2 * E * C * (K * H + H * N)
+
+F32 = mybir.dt.float32
+BF16 = mybir.dt.bfloat16
+U32 = mybir.dt.uint32
+U16 = mybir.dt.uint16
+U8 = mybir.dt.uint8
+FP8X4 = mybir.dt.float8_e4m3fn_x4
+MULT = mybir.AluOpType.mult
+ADD = mybir.AluOpType.add
+SILU = mybir.ActivationFunctionType.Silu
+
+P = 128
+PACK = 4
+K_PASS = P * PACK
+PASSES = K // K_PASS
+SLICE = 2 * C
+N_SLICES = E * C // SLICE
+LIST_COLS = SLICE // 16
+NB = N // P
+
+MV1 = 52
+
+
+def tile_routed_moe_kernel(tc, xT, w1, w2, gate, offs, pos1, pos2, out):
+    nc = tc.nc
+    with ExitStack() as ctx:
+        lists = ctx.enter_context(tc.tile_pool(name="lists", bufs=1))
+        keep = ctx.enter_context(tc.tile_pool(name="keep", bufs=1))
+        raw = ctx.enter_context(tc.tile_pool(name="raw", bufs=10))
+        grp = ctx.enter_context(tc.tile_pool(name="grp", bufs=3))
+        wq = ctx.enter_context(tc.tile_pool(name="wq", bufs=3))
+        tok = ctx.enter_context(tc.tile_pool(name="tok", bufs=4))
+        tokg = ctx.enter_context(tc.tile_pool(name="tokg", bufs=2))
+        hid = ctx.enter_context(tc.tile_pool(name="hid", bufs=2))
+        fin = ctx.enter_context(tc.tile_pool(name="fin", bufs=2))
+        psum_a = ctx.enter_context(tc.psum_pool(name="psum_a", bufs=3))
+        psum_y = ctx.enter_context(tc.psum_pool(name="psum_y", bufs=2))
+
+        warm_in = keep.tile([P, 1], F32, name="warm_in")
+        warm_out = keep.tile([P, 1], F32, name="warm_out")
+        nc.vector.memset(warm_in[:], 0.0)
+        nc.scalar.activation(out=warm_out[:], in_=warm_in[:], func=SILU)
+
+        offs_t = lists.tile([P, E * C // 16], U16, name="offs_t")
+        nc.sync.dma_start(offs_t[:], offs)
+        x_view = xT.rearrange("(g p t) n -> g p t n", p=P, t=PACK)
+        planes = []
+        for g in range(PASSES):
+            row = []
+            for t in range(PACK):
+                plane = keep.tile([P, T], F32, name="plane%d%d" % (g, t))
+                nc.sync.dma_start(out=plane[:], in_=x_view[g, :, t, :])
+                row.append(plane)
+            planes.append(row)
+
+        w1_view = w1.rearrange("e (g p j) c -> e g p j c", p=P, j=PACK)
+        w2_view = w2.rearrange("e (p j) n -> p e j n", j=PACK)
+        w1_raw = {}
+        w2_raw = {}
+        pos1_t = lists.tile([P, T // 16], U16, name="pos1_t")
+        pos2_t = lists.tile([P, T // 16], U16, name="pos2_t")
+        for s in range(N_SLICES):
+            for e in (2 * s, 2 * s + 1):
+                for g in range(PASSES):
+                    r1 = raw.tile([P, PACK, H], F32, name="raw")
+                    nc.sync.dma_start(out=r1[:], in_=w1_view[e, g])
+                    w1_raw[(e, g)] = r1
+            r2 = raw.tile([P, 2, PACK * N], F32, name="raw")
+            nc.sync.dma_start(
+                out=r2[:], in_=w2_view[:, 2 * s:2 * s + 2].rearrange("p e j n -> p e (j n)")
+            )
+            w2_raw[s] = r2
+            if s == 0:
+                nc.sync.dma_start(pos1_t[:], pos1)
+                nc.sync.dma_start(pos2_t[:], pos2)
+        gate_t = {}
+        for b in range(NB):
+            for r in range(2):
+                gt = keep.tile([P, T], F32, name="gate%d%d" % (r, b))
+                nc.sync.dma_start(out=gt[:], in_=gate[r, b * P:(b + 1) * P, :])
+                gate_t[(r, b)] = gt
+
+        y_sb = [keep.tile([P, E * C], F32, name="y_sb%d" % b) for b in range(NB)]
+
+        x_grouped = {}
+        x_codes = {}
+
+        def tokens_half(s, g):
+            if g == 0:
+                x_grouped[s] = tokg.tile([P, PASSES, SLICE * PACK], BF16, name="xg", align_bytes=64)
+            g4 = tok.tile([P, PACK, SLICE], F32, name="g4")
+            for t in range(PACK):
+                nc.vector.tensor_copy(
+                    g4[:, t, :],
+                    planes[g][t][:].indirect(offs_t[:, s * LIST_COLS:(s + 1) * LIST_COLS]),
+                )
+            nc.scalar.copy(
+                out=x_grouped[s][:, g, :].rearrange("p (c i t) -> p c t i", i=4, t=PACK),
+                in_=g4[:].rearrange("p t (c i) -> p c t i", i=4),
+            )
+
+        def tokens_quant(s):
+            xc = keep.tile([P, PASSES * SLICE], U32, name="xc%d" % s, align_bytes=64)
+            xs = keep.tile([P, PASSES * SLICE], U8, name="xs%d" % s, align_bytes=64)
+            nc.vector.quantize_mx(
+                out=xc[:].bitcast(FP8X4), scales=xs[:],
+                in_=x_grouped[s][:].rearrange("p g w -> p (g w)"),
+            )
+            x_codes[s] = (xc, xs)
+
+        w1_codes = {}
+        w2_codes = {}
+
+        def weights1(e):
+            wg = grp.tile([P, PASSES, H * PACK], BF16, name="w1g", align_bytes=64)
+            for g in range(PASSES):
+                src = w1_raw[(e, g)][:].rearrange("p j (m t) -> p m j t", t=PACK)
+                dst = wg[:, g, :].rearrange("p (t m j) -> p m j t", t=PACK, j=PACK)
+                nc.vector.tensor_copy(out=dst[:, :MV1], in_=src[:, :MV1])
+                nc.scalar.copy(out=dst[:, MV1:], in_=src[:, MV1:])
+            wc = wq.tile([P, PASSES * H], U32, name="w1c", align_bytes=64)
+            ws = wq.tile([P, PASSES * H], U8, name="w1s", align_bytes=64)
+            nc.vector.quantize_mx(
+                out=wc[:].bitcast(FP8X4), scales=ws[:], in_=wg[:].rearrange("p g w -> p (g w)")
+            )
+            w1_codes[e] = (wc, ws)
+
+        def weights2(s):
+            wg = grp.tile([P, 2, N * PACK], BF16, name="w2g", align_bytes=64)
+            for half in range(2):
+                nc.scalar.copy(
+                    out=wg[:, half, :].rearrange("p (c i j) -> p c j i", i=4, j=PACK),
+                    in_=w2_raw[s][:, half, :].rearrange("p (j c i) -> p c j i", j=PACK, i=4),
+                )
+            wc = wq.tile([P, 2 * N], U32, name="w2c", align_bytes=64)
+            ws = wq.tile([P, 2 * N], U8, name="w2s", align_bytes=64)
+            nc.vector.quantize_mx(
+                out=wc[:].bitcast(FP8X4), scales=ws[:], in_=wg[:].rearrange("p e w -> p (e w)")
+            )
+            w2_codes[s] = (wc, ws)
+
+        h_grouped = {}
+
+        def layer1(e):
+            s, half = e // 2, e % 2
+            if half == 0:
+                h_grouped[s] = hid.tile([P, 2, C * PACK], BF16, name="hg", align_bytes=64)
+            wc, ws = w1_codes[e]
+            xc, xs = x_codes[s]
+            a_ps = psum_a.tile([P, PACK, C], F32, name="a_ps")
+            for t in range(PACK):
+                for g in range(PASSES):
+                    wcol = slice(g * H + t * P, g * H + (t + 1) * P)
+                    xcol = slice(g * SLICE + half * C, g * SLICE + (half + 1) * C)
+                    nc.tensor.matmul_mx(
+                        out=a_ps[:, t, :],
+                        lhsT=wc[:, wcol].bitcast(FP8X4), lhsT_scale=ws[:, wcol],
+                        rhs=xc[:, xcol].bitcast(FP8X4), rhs_scale=xs[:, xcol],
+                        start=(g == 0), stop=(g == PASSES - 1),
+                    )
+            nc.scalar.activation(
+                out=h_grouped[s][:, half, :].rearrange("p (n t) -> p n t", t=PACK),
+                in_=a_ps[:].rearrange("p t n -> p n t"),
+                func=SILU,
+            )
+
+        def layer2(s):
+            hc = hid.tile([P, SLICE], U32, name="hc", align_bytes=64)
+            hs = hid.tile([P, SLICE], U8, name="hs", align_bytes=64)
+            nc.vector.quantize_mx(
+                out=hc[:].bitcast(FP8X4), scales=hs[:],
+                in_=h_grouped[s][:].rearrange("p e w -> p (e w)"),
+            )
+            wc, ws = w2_codes[s]
+            pair = slice(s * SLICE, (s + 1) * SLICE)
+            for b in range(NB):
+                y_ps = psum_y.tile([P, SLICE], F32, name="y_ps%d" % b)
+                for half in range(2):
+                    wcol = slice(half * N + b * P, half * N + (b + 1) * P)
+                    hcol = slice(half * C, (half + 1) * C)
+                    nc.tensor.matmul_mx(
+                        out=y_ps[:, hcol],
+                        lhsT=wc[:, wcol].bitcast(FP8X4), lhsT_scale=ws[:, wcol],
+                        rhs=hc[:, hcol].bitcast(FP8X4), rhs_scale=hs[:, hcol],
+                        start=True, stop=True,
+                    )
+                if b == 0:
+                    nc.vector.tensor_copy(out=y_sb[b][:, pair], in_=y_ps[:])
+                else:
+                    nc.scalar.copy(out=y_sb[b][:, pair], in_=y_ps[:])
+
+        tokens_half(0, 0)
+        tokens_half(0, 1)
+        tokens_quant(0)
+        for s in range(N_SLICES):
+            for e in (2 * s, 2 * s + 1):
+                weights1(e)
+                if s + 1 < N_SLICES:
+                    tokens_half(s + 1, e % 2)
+                layer1(e)
+            weights2(s)
+            if s + 1 < N_SLICES:
+                tokens_quant(s + 1)
+            layer2(s)
+
+        for b in range(NB):
+            g1 = fin.tile([P, T], F32, name="g1")
+            g2 = fin.tile([P, T], F32, name="g2")
+            res = fin.tile([P, T], F32, name="res")
+            nc.vector.tensor_tensor(g1[:], y_sb[b][:].indirect(pos1_t[:]), gate_t[(0, b)][:], MULT)
+            nc.vector.tensor_tensor(g2[:], y_sb[b][:].indirect(pos2_t[:]), gate_t[(1, b)][:], MULT)
+            nc.vector.tensor_tensor(res[:], g1[:], g2[:], ADD)
+            nc.sync.dma_start(out=out[b * P:(b + 1) * P, :], in_=res[:])

@@ -24,7 +24,8 @@ N_SLICES = E * C // SLICE
 LIST_COLS = SLICE // 16
 NB = N // P
 
-MV1 = 52
+V_FROM_EXPERT = 4
+V_FROM_PAIR = 2
 
 
 def tile_routed_moe_kernel(tc, xT, w1, w2, gate, offs, pos1, pos2, out):
@@ -32,13 +33,13 @@ def tile_routed_moe_kernel(tc, xT, w1, w2, gate, offs, pos1, pos2, out):
     with ExitStack() as ctx:
         lists = ctx.enter_context(tc.tile_pool(name="lists", bufs=1))
         keep = ctx.enter_context(tc.tile_pool(name="keep", bufs=1))
-        raw = ctx.enter_context(tc.tile_pool(name="raw", bufs=10))
-        grp = ctx.enter_context(tc.tile_pool(name="grp", bufs=3))
+        raw = ctx.enter_context(tc.tile_pool(name="raw", bufs=8))
+        grp = ctx.enter_context(tc.tile_pool(name="grp", bufs=4))
         wq = ctx.enter_context(tc.tile_pool(name="wq", bufs=3))
-        tok = ctx.enter_context(tc.tile_pool(name="tok", bufs=4))
-        tokg = ctx.enter_context(tc.tile_pool(name="tokg", bufs=2))
+        tok = ctx.enter_context(tc.tile_pool(name="tok", bufs=8))
+        tokg = ctx.enter_context(tc.tile_pool(name="tokg", bufs=4))
         hid = ctx.enter_context(tc.tile_pool(name="hid", bufs=2))
-        fin = ctx.enter_context(tc.tile_pool(name="fin", bufs=2))
+        wide = ctx.enter_context(tc.tile_pool(name="wide", bufs=8))
         psum_a = ctx.enter_context(tc.psum_pool(name="psum_a", bufs=3))
         psum_y = ctx.enter_context(tc.psum_pool(name="psum_y", bufs=2))
 
@@ -50,39 +51,48 @@ def tile_routed_moe_kernel(tc, xT, w1, w2, gate, offs, pos1, pos2, out):
         offs_t = lists.tile([P, E * C // 16], U16, name="offs_t")
         nc.sync.dma_start(offs_t[:], offs)
         x_view = xT.rearrange("(g p t) n -> g p t n", p=P, t=PACK)
-        planes = []
-        for g in range(PASSES):
-            row = []
-            for t in range(PACK):
-                plane = keep.tile([P, T], F32, name="plane%d%d" % (g, t))
-                nc.sync.dma_start(out=plane[:], in_=x_view[g, :, t, :])
-                row.append(plane)
-            planes.append(row)
-
         w1_view = w1.rearrange("e (g p j) c -> e g p j c", p=P, j=PACK)
         w2_view = w2.rearrange("e (p j) n -> p e j n", j=PACK)
         w1_raw = {}
         w2_raw = {}
         pos1_t = lists.tile([P, T // 16], U16, name="pos1_t")
         pos2_t = lists.tile([P, T // 16], U16, name="pos2_t")
+
+        weight_tiles = []
         for s in range(N_SLICES):
             for e in (2 * s, 2 * s + 1):
                 for g in range(PASSES):
-                    r1 = raw.tile([P, PACK, H], F32, name="raw")
-                    nc.sync.dma_start(out=r1[:], in_=w1_view[e, g])
-                    w1_raw[(e, g)] = r1
-            r2 = raw.tile([P, 2, PACK * N], F32, name="raw")
-            nc.sync.dma_start(
-                out=r2[:], in_=w2_view[:, 2 * s:2 * s + 2].rearrange("p e j n -> p e (j n)")
-            )
-            w2_raw[s] = r2
-            if s == 0:
-                nc.sync.dma_start(pos1_t[:], pos1)
-                nc.sync.dma_start(pos2_t[:], pos2)
+                    weight_tiles.append((1, e, g))
+            weight_tiles.append((2, s, 0))
+
+        def load_weight_tile(k):
+            layer, a, g = weight_tiles[k]
+            if layer == 1:
+                r1 = raw.tile([P, PACK, H], F32, name="raw")
+                nc.sync.dma_start(out=r1[:], in_=w1_view[a, g])
+                w1_raw[(a, g)] = r1
+            else:
+                r2 = raw.tile([P, 2, PACK * N], F32, name="raw")
+                nc.sync.dma_start(
+                    out=r2[:], in_=w2_view[:, 2 * a:2 * a + 2].rearrange("p e j n -> p e (j n)")
+                )
+                w2_raw[a] = r2
+
+        planes = [[], []]
+        for k in range(PASSES * PACK):
+            g, t = k // PACK, k % PACK
+            plane = wide.tile([P, T], F32, name="plane%d%d" % (g, t), tag="wide")
+            nc.sync.dma_start(out=plane[:], in_=x_view[g, :, t, :])
+            planes[g].append(plane)
+            load_weight_tile(k)
+        nc.sync.dma_start(pos1_t[:], pos1)
+        nc.sync.dma_start(pos2_t[:], pos2)
+        for k in range(PASSES * PACK, len(weight_tiles)):
+            load_weight_tile(k)
         gate_t = {}
         for b in range(NB):
             for r in range(2):
-                gt = keep.tile([P, T], F32, name="gate%d%d" % (r, b))
+                gt = wide.tile([P, T], F32, name="gate%d%d" % (r, b), tag="wide")
                 nc.sync.dma_start(out=gt[:], in_=gate[r, b * P:(b + 1) * P, :])
                 gate_t[(r, b)] = gt
 
@@ -91,19 +101,25 @@ def tile_routed_moe_kernel(tc, xT, w1, w2, gate, offs, pos1, pos2, out):
         x_grouped = {}
         x_codes = {}
 
-        def tokens_half(s, g):
-            if g == 0:
-                x_grouped[s] = tokg.tile([P, PASSES, SLICE * PACK], BF16, name="xg", align_bytes=64)
-            g4 = tok.tile([P, PACK, SLICE], F32, name="g4")
+        def tokens_pass(g):
+            g4s = []
+            for s in range(N_SLICES):
+                if g == 0:
+                    x_grouped[s] = tokg.tile([P, PASSES, SLICE * PACK], BF16, name="xg", align_bytes=64)
+                g4 = tok.tile([P, PACK, SLICE], F32, name="g4")
+                g4s.append(g4)
             for t in range(PACK):
-                nc.vector.tensor_copy(
-                    g4[:, t, :],
-                    planes[g][t][:].indirect(offs_t[:, s * LIST_COLS:(s + 1) * LIST_COLS]),
+                for s in range(N_SLICES):
+                    nc.vector.tensor_copy(
+                        g4s[s][:, t, :],
+                        planes[g][t][:].indirect(offs_t[:, s * LIST_COLS:(s + 1) * LIST_COLS]),
+                    )
+            for s in range(N_SLICES):
+                nc.gpsimd.tensor_scalar(
+                    out=x_grouped[s][:, g, :].rearrange("p (n t) -> p n t", t=PACK),
+                    in0=g4s[s][:].rearrange("p t n -> p n t"),
+                    scalar1=1.0, scalar2=0.0, op0=MULT, op1=ADD,
                 )
-            nc.scalar.copy(
-                out=x_grouped[s][:, g, :].rearrange("p (c i t) -> p c t i", i=4, t=PACK),
-                in_=g4[:].rearrange("p t (c i) -> p c t i", i=4),
-            )
 
         def tokens_quant(s):
             xc = keep.tile([P, PASSES * SLICE], U32, name="xc%d" % s, align_bytes=64)
@@ -122,8 +138,10 @@ def tile_routed_moe_kernel(tc, xT, w1, w2, gate, offs, pos1, pos2, out):
             for g in range(PASSES):
                 src = w1_raw[(e, g)][:].rearrange("p j (m t) -> p m j t", t=PACK)
                 dst = wg[:, g, :].rearrange("p (t m j) -> p m j t", t=PACK, j=PACK)
-                nc.vector.tensor_copy(out=dst[:, :MV1], in_=src[:, :MV1])
-                nc.scalar.copy(out=dst[:, MV1:], in_=src[:, MV1:])
+                if g == 1 and e >= V_FROM_EXPERT:
+                    nc.vector.tensor_copy(out=dst, in_=src)
+                else:
+                    nc.scalar.copy(out=dst, in_=src)
             wc = wq.tile([P, PASSES * H], U32, name="w1c", align_bytes=64)
             ws = wq.tile([P, PASSES * H], U8, name="w1s", align_bytes=64)
             nc.vector.quantize_mx(
@@ -134,10 +152,12 @@ def tile_routed_moe_kernel(tc, xT, w1, w2, gate, offs, pos1, pos2, out):
         def weights2(s):
             wg = grp.tile([P, 2, N * PACK], BF16, name="w2g", align_bytes=64)
             for half in range(2):
-                nc.scalar.copy(
-                    out=wg[:, half, :].rearrange("p (c i j) -> p c j i", i=4, j=PACK),
-                    in_=w2_raw[s][:, half, :].rearrange("p (j c i) -> p c j i", j=PACK, i=4),
-                )
+                dst = wg[:, half, :].rearrange("p (c i j) -> p c j i", i=4, j=PACK)
+                src = w2_raw[s][:, half, :].rearrange("p (j c i) -> p c j i", j=PACK, i=4)
+                if s >= V_FROM_PAIR:
+                    nc.vector.tensor_copy(out=dst, in_=src)
+                else:
+                    nc.scalar.copy(out=dst, in_=src)
             wc = wq.tile([P, 2 * N], U32, name="w2c", align_bytes=64)
             ws = wq.tile([P, 2 * N], U8, name="w2s", align_bytes=64)
             nc.vector.quantize_mx(
@@ -146,11 +166,13 @@ def tile_routed_moe_kernel(tc, xT, w1, w2, gate, offs, pos1, pos2, out):
             w2_codes[s] = (wc, ws)
 
         h_grouped = {}
+        GROUP = 4
 
         def layer1(e):
             s, half = e // 2, e % 2
-            if half == 0:
-                h_grouped[s] = hid.tile([P, 2, C * PACK], BF16, name="hg", align_bytes=64)
+            q, i = e // GROUP, e % GROUP
+            if i == 0:
+                h_grouped[q] = hid.tile([P, GROUP, C * PACK], BF16, name="hg", align_bytes=64)
             wc, ws = w1_codes[e]
             xc, xs = x_codes[s]
             a_ps = psum_a.tile([P, PACK, C], F32, name="a_ps")
@@ -165,54 +187,53 @@ def tile_routed_moe_kernel(tc, xT, w1, w2, gate, offs, pos1, pos2, out):
                         start=(g == 0), stop=(g == PASSES - 1),
                     )
             nc.scalar.activation(
-                out=h_grouped[s][:, half, :].rearrange("p (n t) -> p n t", t=PACK),
+                out=h_grouped[q][:, i, :].rearrange("p (n t) -> p n t", t=PACK),
                 in_=a_ps[:].rearrange("p t n -> p n t"),
                 func=SILU,
             )
 
-        def layer2(s):
-            hc = hid.tile([P, SLICE], U32, name="hc", align_bytes=64)
-            hs = hid.tile([P, SLICE], U8, name="hs", align_bytes=64)
+        def layer2(q):
+            hc = hid.tile([P, GROUP * C], U32, name="hc", align_bytes=64)
+            hs = hid.tile([P, GROUP * C], U8, name="hs", align_bytes=64)
             nc.vector.quantize_mx(
                 out=hc[:].bitcast(FP8X4), scales=hs[:],
-                in_=h_grouped[s][:].rearrange("p e w -> p (e w)"),
+                in_=h_grouped[q][:].rearrange("p e w -> p (e w)"),
             )
-            wc, ws = w2_codes[s]
-            pair = slice(s * SLICE, (s + 1) * SLICE)
+            cols = slice(q * GROUP * C, (q + 1) * GROUP * C)
             for b in range(NB):
-                y_ps = psum_y.tile([P, SLICE], F32, name="y_ps%d" % b)
-                for half in range(2):
-                    wcol = slice(half * N + b * P, half * N + (b + 1) * P)
-                    hcol = slice(half * C, (half + 1) * C)
+                y_ps = psum_y.tile([P, GROUP * C], F32, name="y_ps%d" % b)
+                for i in range(GROUP):
+                    e = q * GROUP + i
+                    wc, ws = w2_codes[e // 2]
+                    wcol = slice((e % 2) * N + b * P, (e % 2) * N + (b + 1) * P)
+                    hcol = slice(i * C, (i + 1) * C)
                     nc.tensor.matmul_mx(
                         out=y_ps[:, hcol],
                         lhsT=wc[:, wcol].bitcast(FP8X4), lhsT_scale=ws[:, wcol],
                         rhs=hc[:, hcol].bitcast(FP8X4), rhs_scale=hs[:, hcol],
                         start=True, stop=True,
                     )
-                if b == 0:
-                    nc.vector.tensor_copy(out=y_sb[b][:, pair], in_=y_ps[:])
+                if b == 0 and q == E // GROUP - 1:
+                    nc.vector.tensor_copy(out=y_sb[b][:, cols], in_=y_ps[:])
                 else:
-                    nc.scalar.copy(out=y_sb[b][:, pair], in_=y_ps[:])
+                    nc.scalar.copy(out=y_sb[b][:, cols], in_=y_ps[:])
 
-        tokens_half(0, 0)
-        tokens_half(0, 1)
-        tokens_quant(0)
+        tokens_pass(0)
+        tokens_pass(1)
+        for s in range(N_SLICES):
+            tokens_quant(s)
         for s in range(N_SLICES):
             for e in (2 * s, 2 * s + 1):
                 weights1(e)
-                if s + 1 < N_SLICES:
-                    tokens_half(s + 1, e % 2)
                 layer1(e)
             weights2(s)
-            if s + 1 < N_SLICES:
-                tokens_quant(s + 1)
-            layer2(s)
+            if s % 2 == 1:
+                layer2(s // 2)
 
         for b in range(NB):
-            g1 = fin.tile([P, T], F32, name="g1")
-            g2 = fin.tile([P, T], F32, name="g2")
-            res = fin.tile([P, T], F32, name="res")
+            g1 = wide.tile([P, T], F32, name="g1", tag="wide")
+            g2 = wide.tile([P, T], F32, name="g2", tag="wide")
+            res = wide.tile([P, T], F32, name="res", tag="wide")
             nc.vector.tensor_tensor(g1[:], y_sb[b][:].indirect(pos1_t[:]), gate_t[(0, b)][:], MULT)
             nc.vector.tensor_tensor(g2[:], y_sb[b][:].indirect(pos2_t[:]), gate_t[(1, b)][:], MULT)
             nc.vector.tensor_tensor(res[:], g1[:], g2[:], ADD)

@@ -55,15 +55,22 @@ def tile_routed_moe_kernel(tc, xT, w1, w2, gate, offs, pos1, pos2, out):
         w2_view = w2.rearrange("e (p j) n -> p e j n", j=PACK)
         w1_raw = {}
         w2_raw = {}
+        w2_single_raw = {}
         pos1_t = lists.tile([P, T // 16], U16, name="pos1_t")
         pos2_t = lists.tile([P, T // 16], U16, name="pos2_t")
 
         weight_tiles = []
-        for s in range(N_SLICES):
+        for s in range(2):
             for e in (2 * s, 2 * s + 1):
                 for g in range(PASSES):
                     weight_tiles.append((1, e, g))
             weight_tiles.append((2, s, 0))
+        for e in range(4, E):
+            for g in range(PASSES):
+                weight_tiles.append((1, e, g))
+        weight_tiles.append((2, 2, 0))
+        weight_tiles.append((3, 6, 0))
+        weight_tiles.append((3, 7, 0))
 
         def load_weight_tile(k):
             layer, a, g = weight_tiles[k]
@@ -71,12 +78,16 @@ def tile_routed_moe_kernel(tc, xT, w1, w2, gate, offs, pos1, pos2, out):
                 r1 = raw.tile([P, PACK, H], F32, name="raw")
                 nc.sync.dma_start(out=r1[:], in_=w1_view[a, g])
                 w1_raw[(a, g)] = r1
-            else:
+            elif layer == 2:
                 r2 = raw.tile([P, 2, PACK * N], F32, name="raw")
                 nc.sync.dma_start(
                     out=r2[:], in_=w2_view[:, 2 * a:2 * a + 2].rearrange("p e j n -> p e (j n)")
                 )
                 w2_raw[a] = r2
+            else:
+                r3 = raw.tile([P, PACK * N], F32, name="raw")
+                nc.sync.dma_start(out=r3[:], in_=w2_view[:, a].rearrange("p j n -> p (j n)"))
+                w2_single_raw[a] = r3
 
         planes = [[], []]
         for k in range(PASSES * PACK):
@@ -144,35 +155,63 @@ def tile_routed_moe_kernel(tc, xT, w1, w2, gate, offs, pos1, pos2, out):
                     nc.scalar.copy(out=dst, in_=src)
             wc = wq.tile([P, PASSES * H], U32, name="w1c", align_bytes=64)
             ws = wq.tile([P, PASSES * H], U8, name="w1s", align_bytes=64)
-            nc.vector.quantize_mx(
-                out=wc[:].bitcast(FP8X4), scales=ws[:], in_=wg[:].rearrange("p g w -> p (g w)")
-            )
+            if e == E - 1:
+                for g in range(PASSES):
+                    nc.vector.quantize_mx(
+                        out=wc[:, g * H:(g + 1) * H].bitcast(FP8X4),
+                        scales=ws[:, g * H:(g + 1) * H], in_=wg[:, g, :],
+                    )
+            else:
+                nc.vector.quantize_mx(
+                    out=wc[:].bitcast(FP8X4), scales=ws[:], in_=wg[:].rearrange("p g w -> p (g w)")
+                )
             w1_codes[e] = (wc, ws)
 
         def weights2(s):
-            wg = grp.tile([P, 2, N * PACK], BF16, name="w2g", align_bytes=64)
+            wg = grp.tile([P, 2, N * PACK], BF16, name="w2g", align_bytes=64, bufs=2)
             for half in range(2):
-                dst = wg[:, half, :].rearrange("p (c i j) -> p c j i", i=4, j=PACK)
-                src = w2_raw[s][:, half, :].rearrange("p (j c i) -> p c j i", j=PACK, i=4)
                 if s >= V_FROM_PAIR:
-                    nc.vector.tensor_copy(out=dst, in_=src)
+                    nc.vector.tensor_copy(
+                        out=wg[:, half, :].rearrange("p (c i j) -> p c j i", i=4, j=PACK),
+                        in_=w2_raw[s][:, half, :].rearrange("p (j c i) -> p c j i", j=PACK, i=4),
+                    )
                 else:
-                    nc.scalar.copy(out=dst, in_=src)
+                    nc.gpsimd.tensor_scalar(
+                        out=wg[:, half, :].rearrange("p (n j) -> p n j", j=PACK),
+                        in0=w2_raw[s][:, half, :].rearrange("p (j n) -> p n j", j=PACK),
+                        scalar1=1.0, scalar2=0.0, op0=MULT, op1=ADD,
+                    )
             wc = wq.tile([P, 2 * N], U32, name="w2c", align_bytes=64)
             ws = wq.tile([P, 2 * N], U8, name="w2s", align_bytes=64)
             nc.vector.quantize_mx(
                 out=wc[:].bitcast(FP8X4), scales=ws[:], in_=wg[:].rearrange("p e w -> p (e w)")
             )
-            w2_codes[s] = (wc, ws)
+            w2_codes[2 * s] = (wc, ws, 0)
+            w2_codes[2 * s + 1] = (wc, ws, N)
+
+        def weights2_single(e):
+            wg = grp.tile([P, N * PACK], BF16, name="w2g1", align_bytes=64, bufs=2)
+            dst = wg[:].rearrange("p (c i j) -> p c j i", i=4, j=PACK)
+            src = w2_single_raw[e][:].rearrange("p (j c i) -> p c j i", j=PACK, i=4)
+            if e == E - 1:
+                nc.vector.tensor_copy(out=dst, in_=src)
+            else:
+                nc.scalar.copy(out=dst, in_=src)
+            wc = wq.tile([P, N], U32, name="w2c1", align_bytes=64, bufs=2)
+            ws = wq.tile([P, N], U8, name="w2s1", align_bytes=64, bufs=2)
+            nc.vector.quantize_mx(out=wc[:].bitcast(FP8X4), scales=ws[:], in_=wg[:])
+            w2_codes[e] = (wc, ws, 0)
 
         h_grouped = {}
-        GROUP = 4
+        h_codes = {}
+        GROUPS = ((0, 1, 2, 3), (4, 5), (6, 7))
 
         def layer1(e):
             s, half = e // 2, e % 2
-            q, i = e // GROUP, e % GROUP
+            q = [e in grp_q for grp_q in GROUPS].index(True)
+            i = GROUPS[q].index(e)
             if i == 0:
-                h_grouped[q] = hid.tile([P, GROUP, C * PACK], BF16, name="hg", align_bytes=64)
+                h_grouped[q] = hid.tile([P, len(GROUPS[q]), C * PACK], BF16, name="hg", align_bytes=64)
             wc, ws = w1_codes[e]
             xc, xs = x_codes[s]
             a_ps = psum_a.tile([P, PACK, C], F32, name="a_ps")
@@ -192,43 +231,60 @@ def tile_routed_moe_kernel(tc, xT, w1, w2, gate, offs, pos1, pos2, out):
                 func=SILU,
             )
 
-        def layer2(q):
-            hc = hid.tile([P, GROUP * C], U32, name="hc", align_bytes=64)
-            hs = hid.tile([P, GROUP * C], U8, name="hs", align_bytes=64)
+        def h_quant(q):
+            n = len(GROUPS[q])
+            hc = hid.tile([P, n * C], U32, name="hc", align_bytes=64)
+            hs = hid.tile([P, n * C], U8, name="hs", align_bytes=64)
             nc.vector.quantize_mx(
                 out=hc[:].bitcast(FP8X4), scales=hs[:],
                 in_=h_grouped[q][:].rearrange("p e w -> p (e w)"),
             )
-            cols = slice(q * GROUP * C, (q + 1) * GROUP * C)
-            for b in range(NB):
-                y_ps = psum_y.tile([P, GROUP * C], F32, name="y_ps%d" % b)
-                for i in range(GROUP):
-                    e = q * GROUP + i
-                    wc, ws = w2_codes[e // 2]
-                    wcol = slice((e % 2) * N + b * P, (e % 2) * N + (b + 1) * P)
-                    hcol = slice(i * C, (i + 1) * C)
+            h_codes[q] = (hc, hs)
+
+        def layer2(q):
+            n = len(GROUPS[q])
+            hc, hs = h_codes[q]
+            y_ps = [psum_y.tile([P, n * C], F32, name="y_ps%d" % b) for b in range(NB)]
+            for i in range(n):
+                wc, ws, off = w2_codes[GROUPS[q][i]]
+                hcol = slice(i * C, (i + 1) * C)
+                for b in range(NB):
+                    wcol = slice(off + b * P, off + (b + 1) * P)
                     nc.tensor.matmul_mx(
-                        out=y_ps[:, hcol],
+                        out=y_ps[b][:, hcol],
                         lhsT=wc[:, wcol].bitcast(FP8X4), lhsT_scale=ws[:, wcol],
                         rhs=hc[:, hcol].bitcast(FP8X4), rhs_scale=hs[:, hcol],
                         start=True, stop=True,
                     )
-                if b == 0 and q == E // GROUP - 1:
-                    nc.vector.tensor_copy(out=y_sb[b][:, cols], in_=y_ps[:])
+            cols = slice(GROUPS[q][0] * C, (GROUPS[q][-1] + 1) * C)
+            for b in range(NB):
+                if b == 0 and q == len(GROUPS) - 1:
+                    nc.vector.tensor_copy(out=y_sb[b][:, cols], in_=y_ps[b][:])
                 else:
-                    nc.scalar.copy(out=y_sb[b][:, cols], in_=y_ps[:])
+                    nc.scalar.copy(out=y_sb[b][:, cols], in_=y_ps[b][:])
 
         tokens_pass(0)
         tokens_pass(1)
         for s in range(N_SLICES):
             tokens_quant(s)
-        for s in range(N_SLICES):
+        for s in range(2):
             for e in (2 * s, 2 * s + 1):
                 weights1(e)
                 layer1(e)
             weights2(s)
-            if s % 2 == 1:
-                layer2(s // 2)
+        h_quant(0)
+        layer2(0)
+        for e in range(4, E):
+            weights1(e)
+            layer1(e)
+            if e == 5:
+                h_quant(1)
+        weights2(2)
+        layer2(1)
+        weights2_single(6)
+        h_quant(2)
+        weights2_single(7)
+        layer2(2)
 
         for b in range(NB):
             g1 = wide.tile([P, T], F32, name="g1", tag="wide")

@@ -25,6 +25,7 @@ LIST_COLS = SLICE // 16
 NB = N // P
 
 V_FROM_EXPERT = 4
+PIECE = 64
 V_FROM_PAIR = 2
 
 
@@ -55,22 +56,15 @@ def tile_routed_moe_kernel(tc, xT, w1, w2, gate, offs, pos1, pos2, out):
         w2_view = w2.rearrange("e (p j) n -> p e j n", j=PACK)
         w1_raw = {}
         w2_raw = {}
-        w2_single_raw = {}
         pos1_t = lists.tile([P, T // 16], U16, name="pos1_t")
         pos2_t = lists.tile([P, T // 16], U16, name="pos2_t")
 
         weight_tiles = []
-        for s in range(2):
+        for s in range(N_SLICES):
             for e in (2 * s, 2 * s + 1):
                 for g in range(PASSES):
                     weight_tiles.append((1, e, g))
             weight_tiles.append((2, s, 0))
-        for e in range(4, E):
-            for g in range(PASSES):
-                weight_tiles.append((1, e, g))
-        weight_tiles.append((2, 2, 0))
-        weight_tiles.append((3, 6, 0))
-        weight_tiles.append((3, 7, 0))
 
         def load_weight_tile(k):
             layer, a, g = weight_tiles[k]
@@ -78,16 +72,12 @@ def tile_routed_moe_kernel(tc, xT, w1, w2, gate, offs, pos1, pos2, out):
                 r1 = raw.tile([P, PACK, H], F32, name="raw")
                 nc.sync.dma_start(out=r1[:], in_=w1_view[a, g])
                 w1_raw[(a, g)] = r1
-            elif layer == 2:
+            else:
                 r2 = raw.tile([P, 2, PACK * N], F32, name="raw")
                 nc.sync.dma_start(
                     out=r2[:], in_=w2_view[:, 2 * a:2 * a + 2].rearrange("p e j n -> p e (j n)")
                 )
                 w2_raw[a] = r2
-            else:
-                r3 = raw.tile([P, PACK * N], F32, name="raw")
-                nc.sync.dma_start(out=r3[:], in_=w2_view[:, a].rearrange("p j n -> p (j n)"))
-                w2_single_raw[a] = r3
 
         planes = [[], []]
         for k in range(PASSES * PACK):
@@ -126,11 +116,14 @@ def tile_routed_moe_kernel(tc, xT, w1, w2, gate, offs, pos1, pos2, out):
                         planes[g][t][:].indirect(offs_t[:, s * LIST_COLS:(s + 1) * LIST_COLS]),
                     )
             for s in range(N_SLICES):
-                nc.gpsimd.tensor_scalar(
-                    out=x_grouped[s][:, g, :].rearrange("p (n t) -> p n t", t=PACK),
-                    in0=g4s[s][:].rearrange("p t n -> p n t"),
-                    scalar1=1.0, scalar2=0.0, op0=MULT, op1=ADD,
-                )
+                for n0 in range(0, SLICE, PIECE):
+                    nc.gpsimd.tensor_scalar(
+                        out=x_grouped[s][:, g, n0 * PACK:(n0 + PIECE) * PACK].rearrange(
+                            "p (n t) -> p n t", t=PACK
+                        ),
+                        in0=g4s[s][:, :, n0:n0 + PIECE].rearrange("p t n -> p n t"),
+                        scalar1=1.0, scalar2=0.0, op0=MULT, op1=ADD,
+                    )
 
         def tokens_quant(s):
             xc = keep.tile([P, PASSES * SLICE], U32, name="xc%d" % s, align_bytes=64)
@@ -155,63 +148,35 @@ def tile_routed_moe_kernel(tc, xT, w1, w2, gate, offs, pos1, pos2, out):
                     nc.scalar.copy(out=dst, in_=src)
             wc = wq.tile([P, PASSES * H], U32, name="w1c", align_bytes=64)
             ws = wq.tile([P, PASSES * H], U8, name="w1s", align_bytes=64)
-            if e == E - 1:
-                for g in range(PASSES):
-                    nc.vector.quantize_mx(
-                        out=wc[:, g * H:(g + 1) * H].bitcast(FP8X4),
-                        scales=ws[:, g * H:(g + 1) * H], in_=wg[:, g, :],
-                    )
-            else:
-                nc.vector.quantize_mx(
-                    out=wc[:].bitcast(FP8X4), scales=ws[:], in_=wg[:].rearrange("p g w -> p (g w)")
-                )
+            nc.vector.quantize_mx(
+                out=wc[:].bitcast(FP8X4), scales=ws[:], in_=wg[:].rearrange("p g w -> p (g w)")
+            )
             w1_codes[e] = (wc, ws)
 
         def weights2(s):
-            wg = grp.tile([P, 2, N * PACK], BF16, name="w2g", align_bytes=64, bufs=2)
+            wg = grp.tile([P, 2, N * PACK], BF16, name="w2g", align_bytes=64)
             for half in range(2):
+                dst = wg[:, half, :].rearrange("p (c i j) -> p c j i", i=4, j=PACK)
+                src = w2_raw[s][:, half, :].rearrange("p (j c i) -> p c j i", j=PACK, i=4)
                 if s >= V_FROM_PAIR:
-                    nc.vector.tensor_copy(
-                        out=wg[:, half, :].rearrange("p (c i j) -> p c j i", i=4, j=PACK),
-                        in_=w2_raw[s][:, half, :].rearrange("p (j c i) -> p c j i", j=PACK, i=4),
-                    )
+                    nc.vector.tensor_copy(out=dst, in_=src)
                 else:
-                    nc.gpsimd.tensor_scalar(
-                        out=wg[:, half, :].rearrange("p (n j) -> p n j", j=PACK),
-                        in0=w2_raw[s][:, half, :].rearrange("p (j n) -> p n j", j=PACK),
-                        scalar1=1.0, scalar2=0.0, op0=MULT, op1=ADD,
-                    )
+                    nc.scalar.copy(out=dst, in_=src)
             wc = wq.tile([P, 2 * N], U32, name="w2c", align_bytes=64)
             ws = wq.tile([P, 2 * N], U8, name="w2s", align_bytes=64)
             nc.vector.quantize_mx(
                 out=wc[:].bitcast(FP8X4), scales=ws[:], in_=wg[:].rearrange("p e w -> p (e w)")
             )
-            w2_codes[2 * s] = (wc, ws, 0)
-            w2_codes[2 * s + 1] = (wc, ws, N)
-
-        def weights2_single(e):
-            wg = grp.tile([P, N * PACK], BF16, name="w2g1", align_bytes=64, bufs=2)
-            dst = wg[:].rearrange("p (c i j) -> p c j i", i=4, j=PACK)
-            src = w2_single_raw[e][:].rearrange("p (j c i) -> p c j i", j=PACK, i=4)
-            if e == E - 1:
-                nc.vector.tensor_copy(out=dst, in_=src)
-            else:
-                nc.scalar.copy(out=dst, in_=src)
-            wc = wq.tile([P, N], U32, name="w2c1", align_bytes=64, bufs=2)
-            ws = wq.tile([P, N], U8, name="w2s1", align_bytes=64, bufs=2)
-            nc.vector.quantize_mx(out=wc[:].bitcast(FP8X4), scales=ws[:], in_=wg[:])
-            w2_codes[e] = (wc, ws, 0)
+            w2_codes[s] = (wc, ws)
 
         h_grouped = {}
-        h_codes = {}
-        GROUPS = ((0, 1, 2, 3), (4, 5), (6, 7))
+        GROUP = 4
 
         def layer1(e):
             s, half = e // 2, e % 2
-            q = [e in grp_q for grp_q in GROUPS].index(True)
-            i = GROUPS[q].index(e)
+            q, i = e // GROUP, e % GROUP
             if i == 0:
-                h_grouped[q] = hid.tile([P, len(GROUPS[q]), C * PACK], BF16, name="hg", align_bytes=64)
+                h_grouped[q] = hid.tile([P, GROUP, C * PACK], BF16, name="hg", align_bytes=64)
             wc, ws = w1_codes[e]
             xc, xs = x_codes[s]
             a_ps = psum_a.tile([P, PACK, C], F32, name="a_ps")
@@ -231,60 +196,43 @@ def tile_routed_moe_kernel(tc, xT, w1, w2, gate, offs, pos1, pos2, out):
                 func=SILU,
             )
 
-        def h_quant(q):
-            n = len(GROUPS[q])
-            hc = hid.tile([P, n * C], U32, name="hc", align_bytes=64)
-            hs = hid.tile([P, n * C], U8, name="hs", align_bytes=64)
+        def layer2(q):
+            hc = hid.tile([P, GROUP * C], U32, name="hc", align_bytes=64)
+            hs = hid.tile([P, GROUP * C], U8, name="hs", align_bytes=64)
             nc.vector.quantize_mx(
                 out=hc[:].bitcast(FP8X4), scales=hs[:],
                 in_=h_grouped[q][:].rearrange("p e w -> p (e w)"),
             )
-            h_codes[q] = (hc, hs)
-
-        def layer2(q):
-            n = len(GROUPS[q])
-            hc, hs = h_codes[q]
-            y_ps = [psum_y.tile([P, n * C], F32, name="y_ps%d" % b) for b in range(NB)]
-            for i in range(n):
-                wc, ws, off = w2_codes[GROUPS[q][i]]
-                hcol = slice(i * C, (i + 1) * C)
-                for b in range(NB):
-                    wcol = slice(off + b * P, off + (b + 1) * P)
+            cols = slice(q * GROUP * C, (q + 1) * GROUP * C)
+            for b in range(NB):
+                y_ps = psum_y.tile([P, GROUP * C], F32, name="y_ps%d" % b)
+                for i in range(GROUP):
+                    e = q * GROUP + i
+                    wc, ws = w2_codes[e // 2]
+                    wcol = slice((e % 2) * N + b * P, (e % 2) * N + (b + 1) * P)
+                    hcol = slice(i * C, (i + 1) * C)
                     nc.tensor.matmul_mx(
-                        out=y_ps[b][:, hcol],
+                        out=y_ps[:, hcol],
                         lhsT=wc[:, wcol].bitcast(FP8X4), lhsT_scale=ws[:, wcol],
                         rhs=hc[:, hcol].bitcast(FP8X4), rhs_scale=hs[:, hcol],
                         start=True, stop=True,
                     )
-            cols = slice(GROUPS[q][0] * C, (GROUPS[q][-1] + 1) * C)
-            for b in range(NB):
-                if b == 0 and q == len(GROUPS) - 1:
-                    nc.vector.tensor_copy(out=y_sb[b][:, cols], in_=y_ps[b][:])
+                if b == 0 and q == E // GROUP - 1:
+                    nc.vector.tensor_copy(out=y_sb[b][:, cols], in_=y_ps[:])
                 else:
-                    nc.scalar.copy(out=y_sb[b][:, cols], in_=y_ps[b][:])
+                    nc.scalar.copy(out=y_sb[b][:, cols], in_=y_ps[:])
 
         tokens_pass(0)
         tokens_pass(1)
         for s in range(N_SLICES):
             tokens_quant(s)
-        for s in range(2):
+        for s in range(N_SLICES):
             for e in (2 * s, 2 * s + 1):
                 weights1(e)
                 layer1(e)
             weights2(s)
-        h_quant(0)
-        layer2(0)
-        for e in range(4, E):
-            weights1(e)
-            layer1(e)
-            if e == 5:
-                h_quant(1)
-        weights2(2)
-        layer2(1)
-        weights2_single(6)
-        h_quant(2)
-        weights2_single(7)
-        layer2(2)
+            if s % 2 == 1:
+                layer2(s // 2)
 
         for b in range(NB):
             g1 = wide.tile([P, T], F32, name="g1", tag="wide")

@@ -25,7 +25,6 @@ LIST_COLS = SLICE // 16
 NB = N // P
 
 V_FROM_EXPERT = 4
-PIECE = 64
 V_FROM_PAIR = 2
 
 
@@ -115,15 +114,20 @@ def tile_routed_moe_kernel(tc, xT, w1, w2, gate, offs, pos1, pos2, out):
                         g4s[s][:, t, :],
                         planes[g][t][:].indirect(offs_t[:, s * LIST_COLS:(s + 1) * LIST_COLS]),
                     )
-            for s in range(N_SLICES):
-                for n0 in range(0, SLICE, PIECE):
+            if g == 0:
+                for s in range(N_SLICES):
                     nc.gpsimd.tensor_scalar(
-                        out=x_grouped[s][:, g, n0 * PACK:(n0 + PIECE) * PACK].rearrange(
-                            "p (n t) -> p n t", t=PACK
-                        ),
-                        in0=g4s[s][:, :, n0:n0 + PIECE].rearrange("p t n -> p n t"),
+                        out=x_grouped[s][:, g, :].rearrange("p (n t) -> p n t", t=PACK),
+                        in0=g4s[s][:].rearrange("p t n -> p n t"),
                         scalar1=1.0, scalar2=0.0, op0=MULT, op1=ADD,
                     )
+            return g4s
+
+        def tokens_copy_last(s, g4):
+            nc.vector.tensor_copy(
+                out=x_grouped[s][:, PASSES - 1, :].rearrange("p (c i t) -> p c t i", i=4, t=PACK),
+                in_=g4[:].rearrange("p t (c i) -> p c t i", i=4),
+            )
 
         def tokens_quant(s):
             xc = keep.tile([P, PASSES * SLICE], U32, name="xc%d" % s, align_bytes=64)
@@ -223,9 +227,12 @@ def tile_routed_moe_kernel(tc, xT, w1, w2, gate, offs, pos1, pos2, out):
                     nc.scalar.copy(out=y_sb[b][:, cols], in_=y_ps[:])
 
         tokens_pass(0)
-        tokens_pass(1)
-        for s in range(N_SLICES):
-            tokens_quant(s)
+        last = tokens_pass(1)
+        tokens_copy_last(0, last[0])
+        for s in range(1, N_SLICES):
+            tokens_copy_last(s, last[s])
+            tokens_quant(s - 1)
+        tokens_quant(N_SLICES - 1)
         for s in range(N_SLICES):
             for e in (2 * s, 2 * s + 1):
                 weights1(e)

@@ -14,18 +14,22 @@ FP8X4 = mybir.dt.float8_e4m3fn_x4
 MULT = mybir.AluOpType.mult
 ADD = mybir.AluOpType.add
 SILU = mybir.ActivationFunctionType.Silu
+COPY = mybir.ActivationFunctionType.Copy
 
 P = 128
 PACK = 4
-K_PASS = P * PACK
-PASSES = K // K_PASS
-SLICE = 2 * C
-N_SLICES = E * C // SLICE
-LIST_COLS = SLICE // 16
+PASSES = 2
+LIST_COLS = C // 16
 NB = N // P
+PAIRS = E // 2
+W1_COLS = H * PACK
+X_COLS = PASSES * C * PACK
+W2_COLS = N * PACK
+H_COLS = C * PACK
+FULL = 4096
+HALF = 2048
 
-V_FROM_EXPERT = 4
-V_FROM_PAIR = 2
+SCALAR_W1 = ((6, 0),)
 
 
 def tile_routed_moe_kernel(tc, xT, w1, w2, gate, offs, pos1, pos2, out):
@@ -34,12 +38,11 @@ def tile_routed_moe_kernel(tc, xT, w1, w2, gate, offs, pos1, pos2, out):
         lists = ctx.enter_context(tc.tile_pool(name="lists", bufs=1))
         keep = ctx.enter_context(tc.tile_pool(name="keep", bufs=1))
         raw = ctx.enter_context(tc.tile_pool(name="raw", bufs=8))
-        grp = ctx.enter_context(tc.tile_pool(name="grp", bufs=4))
-        wq = ctx.enter_context(tc.tile_pool(name="wq", bufs=3))
-        tok = ctx.enter_context(tc.tile_pool(name="tok", bufs=8))
-        tokg = ctx.enter_context(tc.tile_pool(name="tokg", bufs=4))
-        hid = ctx.enter_context(tc.tile_pool(name="hid", bufs=2))
-        wide = ctx.enter_context(tc.tile_pool(name="wide", bufs=8))
+        st2 = ctx.enter_context(tc.tile_pool(name="st2", bufs=2))
+        st3 = ctx.enter_context(tc.tile_pool(name="st3", bufs=3))
+        cq2 = ctx.enter_context(tc.tile_pool(name="cq2", bufs=2))
+        cq4 = ctx.enter_context(tc.tile_pool(name="cq4", bufs=3))
+        wide = ctx.enter_context(tc.tile_pool(name="wide", bufs=10))
         psum_a = ctx.enter_context(tc.psum_pool(name="psum_a", bufs=3))
         psum_y = ctx.enter_context(tc.psum_pool(name="psum_y", bufs=2))
 
@@ -50,45 +53,46 @@ def tile_routed_moe_kernel(tc, xT, w1, w2, gate, offs, pos1, pos2, out):
 
         offs_t = lists.tile([P, E * C // 16], U16, name="offs_t")
         nc.sync.dma_start(offs_t[:], offs)
+        pos1_t = lists.tile([P, T // 16], U16, name="pos1_t")
+        pos2_t = lists.tile([P, T // 16], U16, name="pos2_t")
         x_view = xT.rearrange("(g p t) n -> g p t n", p=P, t=PACK)
         w1_view = w1.rearrange("e (g p j) c -> e g p j c", p=P, j=PACK)
         w2_view = w2.rearrange("e (p j) n -> p e j n", j=PACK)
+        x_raw = []
         w1_raw = {}
         w2_raw = {}
-        pos1_t = lists.tile([P, T // 16], U16, name="pos1_t")
-        pos2_t = lists.tile([P, T // 16], U16, name="pos2_t")
 
-        weight_tiles = []
-        for s in range(N_SLICES):
-            for e in (2 * s, 2 * s + 1):
-                for g in range(PASSES):
-                    weight_tiles.append((1, e, g))
-            weight_tiles.append((2, s, 0))
-
-        def load_weight_tile(k):
-            layer, a, g = weight_tiles[k]
-            if layer == 1:
+        def load_w1(e):
+            for g in range(PASSES):
                 r1 = raw.tile([P, PACK, H], F32, name="raw")
-                nc.sync.dma_start(out=r1[:], in_=w1_view[a, g])
-                w1_raw[(a, g)] = r1
-            else:
-                r2 = raw.tile([P, 2, PACK * N], F32, name="raw")
-                nc.sync.dma_start(
-                    out=r2[:], in_=w2_view[:, 2 * a:2 * a + 2].rearrange("p e j n -> p e (j n)")
-                )
-                w2_raw[a] = r2
+                nc.sync.dma_start(out=r1[:], in_=w1_view[e, g])
+                w1_raw[(e, g)] = r1
 
-        planes = [[], []]
-        for k in range(PASSES * PACK):
-            g, t = k // PACK, k % PACK
-            plane = wide.tile([P, T], F32, name="plane%d%d" % (g, t), tag="wide")
-            nc.sync.dma_start(out=plane[:], in_=x_view[g, :, t, :])
-            planes[g].append(plane)
-            load_weight_tile(k)
+        def load_w2(s):
+            r2 = raw.tile([P, 2, W2_COLS], F32, name="raw")
+            nc.sync.dma_start(out=r2[:], in_=w2_view[:, 2 * s:2 * s + 2].rearrange("p e j n -> p e (j n)"))
+            w2_raw[s] = r2
+
+        for g in range(PASSES):
+            xr = raw.tile([P, PACK, T], F32, name="raw")
+            nc.sync.dma_start(out=xr[:], in_=x_view[g])
+            x_raw.append(xr)
+        load_w2(0)
+        load_w1(0)
+        load_w1(1)
+        load_w2(1)
+        load_w1(2)
+        load_w1(3)
         nc.sync.dma_start(pos1_t[:], pos1)
         nc.sync.dma_start(pos2_t[:], pos2)
-        for k in range(PASSES * PACK, len(weight_tiles)):
-            load_weight_tile(k)
+        for e in range(4, E):
+            load_w1(e)
+        load_w2(2)
+        w2_last = {}
+        for e in (6, 7):
+            r3 = raw.tile([P, W2_COLS], F32, name="raw")
+            nc.sync.dma_start(out=r3[:], in_=w2_view[:, e].rearrange("p j n -> p (j n)"))
+            w2_last[e] = r3
         gate_t = {}
         for b in range(NB):
             for r in range(2):
@@ -98,148 +102,150 @@ def tile_routed_moe_kernel(tc, xT, w1, w2, gate, offs, pos1, pos2, out):
 
         y_sb = [keep.tile([P, E * C], F32, name="y_sb%d" % b) for b in range(NB)]
 
-        x_grouped = {}
-        x_codes = {}
+        x_bf = []
+        for g in range(PASSES):
+            xb = keep.tile([P, PACK, T], BF16, name="x_bf%d" % g)
+            nc.vector.tensor_copy(out=xb[:], in_=x_raw[g][:])
+            x_bf.append(xb)
 
-        def tokens_pass(g):
-            g4s = []
-            for s in range(N_SLICES):
-                if g == 0:
-                    x_grouped[s] = tokg.tile([P, PASSES, SLICE * PACK], BF16, name="xg", align_bytes=64)
-                g4 = tok.tile([P, PACK, SLICE], F32, name="g4")
-                g4s.append(g4)
-            for t in range(PACK):
-                for s in range(N_SLICES):
-                    nc.vector.tensor_copy(
-                        g4s[s][:, t, :],
-                        planes[g][t][:].indirect(offs_t[:, s * LIST_COLS:(s + 1) * LIST_COLS]),
-                    )
-            if g == 0:
-                for s in range(N_SLICES):
-                    nc.gpsimd.tensor_scalar(
-                        out=x_grouped[s][:, g, :].rearrange("p (n t) -> p n t", t=PACK),
-                        in0=g4s[s][:].rearrange("p t n -> p n t"),
-                        scalar1=1.0, scalar2=0.0, op0=MULT, op1=ADD,
-                    )
-            return g4s
+        where = {}
 
-        def tokens_copy_last(s, g4):
-            nc.vector.tensor_copy(
-                out=x_grouped[s][:, PASSES - 1, :].rearrange("p (c i t) -> p c t i", i=4, t=PACK),
-                in_=g4[:].rearrange("p t (c i) -> p c t i", i=4),
-            )
+        def put_w1(stage, off, e, g):
+            src = w1_raw[(e, g)][:].rearrange("p j (m t) -> p m j t", t=PACK)
+            dst = stage[:, off:off + W1_COLS].rearrange("p (t m j) -> p m j t", t=PACK, j=PACK)
+            if (e, g) in SCALAR_W1:
+                nc.scalar.copy(out=dst, in_=src)
+            else:
+                nc.vector.tensor_copy(out=dst, in_=src)
 
-        def tokens_quant(s):
-            xc = keep.tile([P, PASSES * SLICE], U32, name="xc%d" % s, align_bytes=64)
-            xs = keep.tile([P, PASSES * SLICE], U8, name="xs%d" % s, align_bytes=64)
-            nc.vector.quantize_mx(
-                out=xc[:].bitcast(FP8X4), scales=xs[:],
-                in_=x_grouped[s][:].rearrange("p g w -> p (g w)"),
-            )
-            x_codes[s] = (xc, xs)
-
-        w1_codes = {}
-        w2_codes = {}
-
-        def weights1(e):
-            wg = grp.tile([P, PASSES, H * PACK], BF16, name="w1g", align_bytes=64)
+        def put_x(stage, off, e):
             for g in range(PASSES):
-                src = w1_raw[(e, g)][:].rearrange("p j (m t) -> p m j t", t=PACK)
-                dst = wg[:, g, :].rearrange("p (t m j) -> p m j t", t=PACK, j=PACK)
-                if g == 1 and e >= V_FROM_EXPERT:
-                    nc.vector.tensor_copy(out=dst, in_=src)
-                else:
-                    nc.scalar.copy(out=dst, in_=src)
-            wc = wq.tile([P, PASSES * H], U32, name="w1c", align_bytes=64)
-            ws = wq.tile([P, PASSES * H], U8, name="w1s", align_bytes=64)
-            nc.vector.quantize_mx(
-                out=wc[:].bitcast(FP8X4), scales=ws[:], in_=wg[:].rearrange("p g w -> p (g w)")
-            )
-            w1_codes[e] = (wc, ws)
+                dst = stage[:, off + g * H_COLS:off + (g + 1) * H_COLS].rearrange("p (n t) -> p n t", t=PACK)
+                for t in range(PACK):
+                    nc.scalar.activation(
+                        out=dst[:, :, t],
+                        in_=x_bf[g][:, t, :].indirect(offs_t[:, e * LIST_COLS:(e + 1) * LIST_COLS]),
+                        func=COPY,
+                    )
 
-        def weights2(s):
-            wg = grp.tile([P, 2, N * PACK], BF16, name="w2g", align_bytes=64)
-            for half in range(2):
-                dst = wg[:, half, :].rearrange("p (c i j) -> p c j i", i=4, j=PACK)
+        def put_w2(stage, off, s, half, engine):
+            dst = stage[:, off:off + W2_COLS].rearrange("p (c i j) -> p c j i", i=4, j=PACK)
+            if s < 3:
                 src = w2_raw[s][:, half, :].rearrange("p (j c i) -> p c j i", j=PACK, i=4)
-                if s >= V_FROM_PAIR:
-                    nc.vector.tensor_copy(out=dst, in_=src)
-                else:
-                    nc.scalar.copy(out=dst, in_=src)
-            wc = wq.tile([P, 2 * N], U32, name="w2c", align_bytes=64)
-            ws = wq.tile([P, 2 * N], U8, name="w2s", align_bytes=64)
-            nc.vector.quantize_mx(
-                out=wc[:].bitcast(FP8X4), scales=ws[:], in_=wg[:].rearrange("p e w -> p (e w)")
-            )
-            w2_codes[s] = (wc, ws)
+            else:
+                src = w2_last[2 * s + half][:].rearrange("p (j c i) -> p c j i", j=PACK, i=4)
+            if engine == "s":
+                nc.scalar.copy(out=dst, in_=src)
+            else:
+                nc.vector.tensor_copy(out=dst, in_=src)
 
-        h_grouped = {}
-        GROUP = 4
+        def quantise(stage, width, pool, tag, parts):
+            codes = pool.tile([P, width // PACK], U32, name=tag + "c", align_bytes=64)
+            scales = pool.tile([P, width // PACK], U8, name=tag + "s", align_bytes=64)
+            nc.vector.quantize_mx(out=codes[:].bitcast(FP8X4), scales=scales[:], in_=stage[:])
+            for key, off in parts:
+                where[key] = (codes, scales, off // PACK)
 
-        def layer1(e):
-            s, half = e // 2, e % 2
-            q, i = e // GROUP, e % GROUP
-            if i == 0:
-                h_grouped[q] = hid.tile([P, GROUP, C * PACK], BF16, name="hg", align_bytes=64)
-            wc, ws = w1_codes[e]
-            xc, xs = x_codes[s]
+        def operand(key, first, count):
+            codes, scales, base = where[key]
+            cols = slice(base + first, base + first + count)
+            return codes[:, cols].bitcast(FP8X4), scales[:, cols]
+
+        def layer1(e, h_stage, h_off):
             a_ps = psum_a.tile([P, PACK, C], F32, name="a_ps")
             for t in range(PACK):
                 for g in range(PASSES):
-                    wcol = slice(g * H + t * P, g * H + (t + 1) * P)
-                    xcol = slice(g * SLICE + half * C, g * SLICE + (half + 1) * C)
+                    wc, ws = operand(("w1", e, g), t * P, P)
+                    xc, xs = operand(("x", e), g * C, C)
                     nc.tensor.matmul_mx(
-                        out=a_ps[:, t, :],
-                        lhsT=wc[:, wcol].bitcast(FP8X4), lhsT_scale=ws[:, wcol],
-                        rhs=xc[:, xcol].bitcast(FP8X4), rhs_scale=xs[:, xcol],
+                        out=a_ps[:, t, :], lhsT=wc, lhsT_scale=ws, rhs=xc, rhs_scale=xs,
                         start=(g == 0), stop=(g == PASSES - 1),
                     )
             nc.scalar.activation(
-                out=h_grouped[q][:, i, :].rearrange("p (n t) -> p n t", t=PACK),
+                out=h_stage[:, h_off:h_off + H_COLS].rearrange("p (n t) -> p n t", t=PACK),
                 in_=a_ps[:].rearrange("p t n -> p n t"),
                 func=SILU,
             )
 
-        def layer2(q):
-            hc = hid.tile([P, GROUP * C], U32, name="hc", align_bytes=64)
-            hs = hid.tile([P, GROUP * C], U8, name="hs", align_bytes=64)
-            nc.vector.quantize_mx(
-                out=hc[:].bitcast(FP8X4), scales=hs[:],
-                in_=h_grouped[q][:].rearrange("p e w -> p (e w)"),
-            )
-            cols = slice(q * GROUP * C, (q + 1) * GROUP * C)
+        def layer2(experts, vector_block):
+            first = experts[0]
+            cols = slice(first * C, (first + len(experts)) * C)
             for b in range(NB):
-                y_ps = psum_y.tile([P, GROUP * C], F32, name="y_ps%d" % b)
-                for i in range(GROUP):
-                    e = q * GROUP + i
-                    wc, ws = w2_codes[e // 2]
-                    wcol = slice((e % 2) * N + b * P, (e % 2) * N + (b + 1) * P)
-                    hcol = slice(i * C, (i + 1) * C)
+                y_ps = psum_y.tile([P, len(experts) * C], F32, name="y_ps%d" % b)
+                for i, e in enumerate(experts):
+                    wc, ws = operand(("w2", e), b * P, P)
+                    hc, hs = operand(("h", e), 0, C)
                     nc.tensor.matmul_mx(
-                        out=y_ps[:, hcol],
-                        lhsT=wc[:, wcol].bitcast(FP8X4), lhsT_scale=ws[:, wcol],
-                        rhs=hc[:, hcol].bitcast(FP8X4), rhs_scale=hs[:, hcol],
+                        out=y_ps[:, i * C:(i + 1) * C], lhsT=wc, lhsT_scale=ws, rhs=hc, rhs_scale=hs,
                         start=True, stop=True,
                     )
-                if b == 0 and q == E // GROUP - 1:
+                if b == vector_block:
                     nc.vector.tensor_copy(out=y_sb[b][:, cols], in_=y_ps[:])
                 else:
                     nc.scalar.copy(out=y_sb[b][:, cols], in_=y_ps[:])
 
-        tokens_pass(0)
-        last = tokens_pass(1)
-        tokens_copy_last(0, last[0])
-        for s in range(1, N_SLICES):
-            tokens_copy_last(s, last[s])
-            tokens_quant(s - 1)
-        tokens_quant(N_SLICES - 1)
-        for s in range(N_SLICES):
-            for e in (2 * s, 2 * s + 1):
-                weights1(e)
-                layer1(e)
-            weights2(s)
-            if s % 2 == 1:
-                layer2(s // 2)
+        c2_stage = {}
+        c3_stage = {}
+
+        def tokens(s):
+            c2_stage[s] = st2.tile([P, FULL], BF16, name="c2", align_bytes=64)
+            put_x(c2_stage[s], W1_COLS, 2 * s)
+            put_x(c2_stage[s], W1_COLS + X_COLS, 2 * s + 1)
+
+        def early_w2(s):
+            c3_stage[s] = st3.tile([P, FULL], BF16, name="c3", align_bytes=64)
+            put_w2(c3_stage[s], W1_COLS, s, 0, "v")
+            put_w2(c3_stage[s], W1_COLS + W2_COLS, s, 1, "v")
+
+        tokens(0)
+        early_w2(0)
+        tokens(1)
+        early_w2(1)
+        c3_stage[2] = st3.tile([P, FULL], BF16, name="c3", align_bytes=64)
+        t1 = keep.tile([P, FULL], BF16, name="t1", align_bytes=64)
+
+        def h_place(e):
+            if e < 4:
+                return c3_stage[2], W1_COLS + e * H_COLS
+            return t1, HALF + (e - 4) * H_COLS
+
+        for s in range(PAIRS):
+            a, b2 = 2 * s, 2 * s + 1
+            c1 = st2.tile([P, FULL], BF16, name="c1", align_bytes=64)
+            put_w1(c1, 0, a, 0)
+            put_w1(c1, W1_COLS, a, 1)
+            quantise(c1, FULL, cq2, "q1", [(("w1", a, 0), 0), (("w1", a, 1), W1_COLS)])
+            put_w1(c2_stage[s], 0, b2, 0)
+            quantise(c2_stage[s], FULL, cq2, "q2",
+                     [(("w1", b2, 0), 0), (("x", a), W1_COLS), (("x", b2), W1_COLS + X_COLS)])
+            layer1(a, *h_place(a))
+            if s + 2 < PAIRS:
+                tokens(s + 2)
+            if s < 3:
+                put_w1(c3_stage[s], 0, b2, 1)
+                if s < 2:
+                    parts = [(("w2", a), W1_COLS), (("w2", b2), W1_COLS + W2_COLS)]
+                else:
+                    parts = [(("h", e), W1_COLS + e * H_COLS) for e in range(4)]
+                quantise(c3_stage[s], FULL, cq4, "q3", [(("w1", b2, 1), 0)] + parts)
+            else:
+                c4 = st2.tile([P, HALF], BF16, name="c4", align_bytes=64)
+                put_w1(c4, 0, b2, 1)
+                quantise(c4, HALF, cq2, "q4", [(("w1", b2, 1), 0)])
+            layer1(b2, *h_place(b2))
+            if s == 2:
+                layer2([0, 1, 2, 3], -1)
+
+        put_w2(t1, 0, 2, 0, "s")
+        put_w2(t1, W2_COLS, 2, 1, "v")
+        quantise(t1, FULL, cq2, "q6",
+                 [(("w2", 4), 0), (("w2", 5), W2_COLS)] + [(("h", e), HALF + (e - 4) * H_COLS) for e in range(4, E)])
+        layer2([4, 5], -1)
+        t2 = st2.tile([P, HALF], BF16, name="c4", align_bytes=64)
+        put_w2(t2, 0, 3, 0, "s")
+        put_w2(t2, W2_COLS, 3, 1, "v")
+        quantise(t2, HALF, cq2, "q5", [(("w2", 6), 0), (("w2", 7), W2_COLS)])
+        layer2([6, 7], 0)
 
         for b in range(NB):
             g1 = wide.tile([P, T], F32, name="g1", tag="wide")

@@ -37,7 +37,7 @@ def tile_routed_moe_kernel(tc, xT, w1, w2, gate, offs, pos1, pos2, out):
     with ExitStack() as ctx:
         lists = ctx.enter_context(tc.tile_pool(name="lists", bufs=1))
         keep = ctx.enter_context(tc.tile_pool(name="keep", bufs=1))
-        raw = ctx.enter_context(tc.tile_pool(name="raw", bufs=8))
+        raw = ctx.enter_context(tc.tile_pool(name="raw", bufs=4))
         st2 = ctx.enter_context(tc.tile_pool(name="st2", bufs=2))
         st3 = ctx.enter_context(tc.tile_pool(name="st3", bufs=3))
         cq2 = ctx.enter_context(tc.tile_pool(name="cq2", bufs=2))

@@ -42,7 +42,7 @@ def tile_routed_moe_kernel(tc, xT, w1, w2, gate, offs, pos1, pos2, out):
         st3 = ctx.enter_context(tc.tile_pool(name="st3", bufs=3))
         cq2 = ctx.enter_context(tc.tile_pool(name="cq2", bufs=2))
         cq4 = ctx.enter_context(tc.tile_pool(name="cq4", bufs=3))
-        wide = ctx.enter_context(tc.tile_pool(name="wide", bufs=10))
+        wide = ctx.enter_context(tc.tile_pool(name="wide", bufs=6))
         psum_a = ctx.enter_context(tc.psum_pool(name="psum_a", bufs=3))
         psum_y = ctx.enter_context(tc.psum_pool(name="psum_y", bufs=2))
 
@@ -52,7 +52,6 @@ def tile_routed_moe_kernel(tc, xT, w1, w2, gate, offs, pos1, pos2, out):
         nc.scalar.activation(out=warm_out[:], in_=warm_in[:], func=SILU)
 
         offs_t = lists.tile([P, E * C // 16], U16, name="offs_t")
-        nc.sync.dma_start(offs_t[:], offs)
         pos1_t = lists.tile([P, T // 16], U16, name="pos1_t")
         pos2_t = lists.tile([P, T // 16], U16, name="pos2_t")
         x_view = xT.rearrange("(g p t) n -> g p t n", p=P, t=PACK)
@@ -77,28 +76,26 @@ def tile_routed_moe_kernel(tc, xT, w1, w2, gate, offs, pos1, pos2, out):
             xr = raw.tile([P, PACK, T], F32, name="raw")
             nc.sync.dma_start(out=xr[:], in_=x_view[g])
             x_raw.append(xr)
+            if g == 0:
+                nc.sync.dma_start(offs_t[:], offs)
         load_w2(0)
         load_w1(0)
         load_w1(1)
-        load_w2(1)
         load_w1(2)
         load_w1(3)
         nc.sync.dma_start(pos1_t[:], pos1)
         nc.sync.dma_start(pos2_t[:], pos2)
         for e in range(4, E):
             load_w1(e)
+        load_w2(1)
         load_w2(2)
         w2_last = {}
         for e in (6, 7):
             r3 = raw.tile([P, W2_COLS], F32, name="raw")
             nc.sync.dma_start(out=r3[:], in_=w2_view[:, e].rearrange("p j n -> p (j n)"))
             w2_last[e] = r3
-        gate_t = {}
-        for b in range(NB):
-            for r in range(2):
-                gt = wide.tile([P, T], F32, name="gate%d%d" % (r, b), tag="wide")
-                nc.sync.dma_start(out=gt[:], in_=gate[r, b * P:(b + 1) * P, :])
-                gate_t[(r, b)] = gt
+        gate_t = keep.tile([P, 2, T], F32, name="gate_t")
+        nc.sync.dma_start(out=gate_t[:], in_=gate[:, 0:P, :].rearrange("r p t -> p r t"))
 
         y_sb = [keep.tile([P, E * C], F32, name="y_sb%d" % b) for b in range(NB)]
 
@@ -200,7 +197,6 @@ def tile_routed_moe_kernel(tc, xT, w1, w2, gate, offs, pos1, pos2, out):
         tokens(0)
         early_w2(0)
         tokens(1)
-        early_w2(1)
         c3_stage[2] = st3.tile([P, FULL], BF16, name="c3", align_bytes=64)
         t1 = keep.tile([P, FULL], BF16, name="t1", align_bytes=64)
 
@@ -221,9 +217,9 @@ def tile_routed_moe_kernel(tc, xT, w1, w2, gate, offs, pos1, pos2, out):
             layer1(a, *h_place(a))
             if s + 2 < PAIRS:
                 tokens(s + 2)
-            if s < 3:
+            if s in (0, 2):
                 put_w1(c3_stage[s], 0, b2, 1)
-                if s < 2:
+                if s == 0:
                     parts = [(("w2", a), W1_COLS), (("w2", b2), W1_COLS + W2_COLS)]
                 else:
                     parts = [(("h", e), W1_COLS + e * H_COLS) for e in range(4)]
@@ -234,24 +230,43 @@ def tile_routed_moe_kernel(tc, xT, w1, w2, gate, offs, pos1, pos2, out):
                 quantise(c4, HALF, cq2, "q4", [(("w1", b2, 1), 0)])
             layer1(b2, *h_place(b2))
             if s == 2:
-                layer2([0, 1, 2, 3], -1)
+                layer2([0, 1], -1)
 
-        put_w2(t1, 0, 2, 0, "s")
-        put_w2(t1, W2_COLS, 2, 1, "v")
+        put_w2(t1, 0, 1, 0, "s")
+        put_w2(t1, W2_COLS, 1, 1, "v")
         quantise(t1, FULL, cq2, "q6",
-                 [(("w2", 4), 0), (("w2", 5), W2_COLS)] + [(("h", e), HALF + (e - 4) * H_COLS) for e in range(4, E)])
+                 [(("w2", 2), 0), (("w2", 3), W2_COLS)] + [(("h", e), HALF + (e - 4) * H_COLS) for e in range(4, E)])
+        layer2([2, 3], -1)
+        t3 = st2.tile([P, HALF], BF16, name="c4", align_bytes=64)
+        put_w2(t3, 0, 2, 0, "s")
+        put_w2(t3, W2_COLS, 2, 1, "v")
+        quantise(t3, HALF, cq2, "q5", [(("w2", 4), 0), (("w2", 5), W2_COLS)])
         layer2([4, 5], -1)
-        t2 = st2.tile([P, HALF], BF16, name="c4", align_bytes=64)
-        put_w2(t2, 0, 3, 0, "s")
-        put_w2(t2, W2_COLS, 3, 1, "v")
-        quantise(t2, HALF, cq2, "q5", [(("w2", 6), 0), (("w2", 7), W2_COLS)])
-        layer2([6, 7], 0)
+        t4 = st2.tile([P, W2_COLS], BF16, name="c5", align_bytes=64)
+        put_w2(t4, 0, 3, 0, "s")
+        quantise(t4, W2_COLS, cq2, "q7", [(("w2", 6), 0)])
+        layer2([6], -1)
+        last = w2_last[7][:].rearrange("p (j c i) -> p c j i", j=PACK, i=4)
+        cols7 = slice(7 * C, 8 * C)
+        for b in range(NB):
+            t5 = st2.tile([P, W2_COLS // NB], BF16, name="c6", align_bytes=64)
+            nc.vector.tensor_copy(
+                out=t5[:].rearrange("p (c i j) -> p c j i", i=4, j=PACK),
+                in_=last[:, b * (P // 4):(b + 1) * (P // 4)],
+            )
+            quantise(t5, W2_COLS // NB, cq2, "q8", [(("w2half", b), 0)])
+        for b in range(NB):
+            y_ps = psum_y.tile([P, C], F32, name="y_ps%d" % b)
+            wc, ws = operand(("w2half", b), 0, P)
+            hc, hs = operand(("h", 7), 0, C)
+            nc.tensor.matmul_mx(out=y_ps[:], lhsT=wc, lhsT_scale=ws, rhs=hc, rhs_scale=hs, start=True, stop=True)
+            nc.scalar.copy(out=y_sb[b][:, cols7], in_=y_ps[:])
 
         for b in range(NB):
             g1 = wide.tile([P, T], F32, name="g1", tag="wide")
             g2 = wide.tile([P, T], F32, name="g2", tag="wide")
             res = wide.tile([P, T], F32, name="res", tag="wide")
-            nc.vector.tensor_tensor(g1[:], y_sb[b][:].indirect(pos1_t[:]), gate_t[(0, b)][:], MULT)
-            nc.vector.tensor_tensor(g2[:], y_sb[b][:].indirect(pos2_t[:]), gate_t[(1, b)][:], MULT)
+            nc.vector.tensor_tensor(g1[:], y_sb[b][:].indirect(pos1_t[:]), gate_t[:, 0, :], MULT)
+            nc.vector.tensor_tensor(g2[:], y_sb[b][:].indirect(pos2_t[:]), gate_t[:, 1, :], MULT)
             nc.vector.tensor_tensor(res[:], g1[:], g2[:], ADD)
             nc.sync.dma_start(out=out[b * P:(b + 1) * P, :], in_=res[:])

@@ -181,29 +181,52 @@ def tile_routed_moe_kernel(tc, xT, w1, w2, gate, offs, pos1, pos2, out):
                 else:
                     nc.scalar.copy(out=y_sb[b][:, cols], in_=y_ps[:])
 
-        c2_stage = {}
-        c3_stage = {}
+        stage = {}
 
-        def tokens(s):
-            c2_stage[s] = st2.tile([P, FULL], BF16, name="c2", align_bytes=64)
-            put_x(c2_stage[s], W1_COLS, 2 * s)
-            put_x(c2_stage[s], W1_COLS + X_COLS, 2 * s + 1)
+        def x_parts(pair):
+            return [(("x", 2 * pair), W1_COLS), (("x", 2 * pair + 1), W1_COLS + X_COLS)]
 
-        def early_w2(s):
-            c3_stage[s] = st3.tile([P, FULL], BF16, name="c3", align_bytes=64)
-            put_w2(c3_stage[s], W1_COLS, s, 0, "v")
-            put_w2(c3_stage[s], W1_COLS + W2_COLS, s, 1, "v")
+        def tokens(pair, key):
+            if key[0] == 2:
+                stage[key] = st2.tile([P, FULL], BF16, name="c2", align_bytes=64)
+            else:
+                stage[key] = st3.tile([P, FULL], BF16, name="c3", align_bytes=64)
+            put_x(stage[key], W1_COLS, 2 * pair)
+            put_x(stage[key], W1_COLS + X_COLS, 2 * pair + 1)
 
-        tokens(0)
-        early_w2(0)
-        tokens(1)
-        c3_stage[2] = st3.tile([P, FULL], BF16, name="c3", align_bytes=64)
+        tokens(0, (2, 0))
+        stage[(3, 0)] = st3.tile([P, FULL], BF16, name="c3", align_bytes=64)
+        put_w2(stage[(3, 0)], W1_COLS, 0, 0, "v")
+        put_w2(stage[(3, 0)], W1_COLS + W2_COLS, 0, 1, "v")
+        tokens(1, (2, 1))
+        tokens(2, (3, 1))
+        stage[(3, 2)] = st3.tile([P, FULL], BF16, name="c3", align_bytes=64)
         t1 = keep.tile([P, FULL], BF16, name="t1", align_bytes=64)
+        extra = {
+            (2, 0): x_parts(0),
+            (2, 1): x_parts(1),
+            (3, 1): x_parts(2),
+            (2, 2): x_parts(3),
+            (3, 0): [(("w2", 0), W1_COLS), (("w2", 1), W1_COLS + W2_COLS)],
+            (3, 2): [(("h", e), W1_COLS + e * H_COLS) for e in range(4)],
+        }
 
         def h_place(e):
             if e < 4:
-                return c3_stage[2], W1_COLS + e * H_COLS
+                return stage[(3, 2)], W1_COLS + e * H_COLS
             return t1, HALF + (e - 4) * H_COLS
+
+        def later_call(key, e, g):
+            if key in extra:
+                put_w1(stage[key], 0, e, g)
+                if key[0] == 2:
+                    quantise(stage[key], FULL, cq2, "q2", [(("w1", e, g), 0)] + extra[key])
+                else:
+                    quantise(stage[key], FULL, cq4, "q3", [(("w1", e, g), 0)] + extra[key])
+            else:
+                c4 = st2.tile([P, HALF], BF16, name="c4", align_bytes=64)
+                put_w1(c4, 0, e, g)
+                quantise(c4, HALF, cq4, "q4", [(("w1", e, g), 0)])
 
         for s in range(PAIRS):
             a, b2 = 2 * s, 2 * s + 1
@@ -211,41 +234,31 @@ def tile_routed_moe_kernel(tc, xT, w1, w2, gate, offs, pos1, pos2, out):
             put_w1(c1, 0, a, 0)
             put_w1(c1, W1_COLS, a, 1)
             quantise(c1, FULL, cq2, "q1", [(("w1", a, 0), 0), (("w1", a, 1), W1_COLS)])
-            put_w1(c2_stage[s], 0, b2, 0)
-            quantise(c2_stage[s], FULL, cq2, "q2",
-                     [(("w1", b2, 0), 0), (("x", a), W1_COLS), (("x", b2), W1_COLS + X_COLS)])
-            layer1(a, *h_place(a))
-            if s + 2 < PAIRS:
-                tokens(s + 2)
-            if s in (0, 2):
-                put_w1(c3_stage[s], 0, b2, 1)
-                if s == 0:
-                    parts = [(("w2", a), W1_COLS), (("w2", b2), W1_COLS + W2_COLS)]
-                else:
-                    parts = [(("h", e), W1_COLS + e * H_COLS) for e in range(4)]
-                quantise(c3_stage[s], FULL, cq4, "q3", [(("w1", b2, 1), 0)] + parts)
-            else:
-                c4 = st2.tile([P, HALF], BF16, name="c4", align_bytes=64)
-                put_w1(c4, 0, b2, 1)
-                quantise(c4, HALF, cq2, "q4", [(("w1", b2, 1), 0)])
+            if s >= 2:
+                layer1(a, *h_place(a))
+            later_call((2, s), b2, 0)
+            if s < 2:
+                layer1(a, *h_place(a))
+            if s == 0:
+                tokens(3, (2, 2))
+            later_call((3, s), b2, 1)
             layer1(b2, *h_place(b2))
             if s == 2:
                 layer2([0, 1], -1)
 
-        put_w2(t1, 0, 1, 0, "s")
-        put_w2(t1, W2_COLS, 1, 1, "v")
-        quantise(t1, FULL, cq2, "q6",
-                 [(("w2", 2), 0), (("w2", 3), W2_COLS)] + [(("h", e), HALF + (e - 4) * H_COLS) for e in range(4, E)])
-        layer2([2, 3], -1)
         t3 = st2.tile([P, HALF], BF16, name="c4", align_bytes=64)
-        put_w2(t3, 0, 2, 0, "s")
-        put_w2(t3, W2_COLS, 2, 1, "v")
-        quantise(t3, HALF, cq2, "q5", [(("w2", 4), 0), (("w2", 5), W2_COLS)])
-        layer2([4, 5], -1)
+        put_w2(t3, 0, 1, 0, "v")
+        put_w2(t3, W2_COLS, 1, 1, "v")
+        quantise(t3, HALF, cq2, "q5", [(("w2", 2), 0), (("w2", 3), W2_COLS)])
+        put_w2(t1, 0, 2, 0, "v")
+        put_w2(t1, W2_COLS, 2, 1, "s")
+        quantise(t1, FULL, cq2, "q6",
+                 [(("w2", 4), 0), (("w2", 5), W2_COLS)] + [(("h", e), HALF + (e - 4) * H_COLS) for e in range(4, E)])
+        layer2([2, 3, 4, 5], -1)
         t4 = st2.tile([P, W2_COLS], BF16, name="c5", align_bytes=64)
         put_w2(t4, 0, 3, 0, "s")
         quantise(t4, W2_COLS, cq2, "q7", [(("w2", 6), 0)])
-        layer2([6], -1)
+        layer2([6], 0)
         last = w2_last[7][:].rearrange("p (j c i) -> p c j i", j=PACK, i=4)
         cols7 = slice(7 * C, 8 * C)
         for b in range(NB):
@@ -260,7 +273,10 @@ def tile_routed_moe_kernel(tc, xT, w1, w2, gate, offs, pos1, pos2, out):
             wc, ws = operand(("w2half", b), 0, P)
             hc, hs = operand(("h", 7), 0, C)
             nc.tensor.matmul_mx(out=y_ps[:], lhsT=wc, lhsT_scale=ws, rhs=hc, rhs_scale=hs, start=True, stop=True)
-            nc.scalar.copy(out=y_sb[b][:, cols7], in_=y_ps[:])
+            if b == 0:
+                nc.vector.tensor_copy(out=y_sb[b][:, cols7], in_=y_ps[:])
+            else:
+                nc.scalar.copy(out=y_sb[b][:, cols7], in_=y_ps[:])
 
         for b in range(NB):
             g1 = wide.tile([P, T], F32, name="g1", tag="wide")

@@ -261,13 +261,16 @@ def tile_routed_moe_kernel(tc, xT, w1, w2, gate, offs, pos1, pos2, out):
         layer2([6], 0)
         last = w2_last[7][:].rearrange("p (j c i) -> p c j i", j=PACK, i=4)
         cols7 = slice(7 * C, 8 * C)
+        halves = []
         for b in range(NB):
             t5 = st2.tile([P, W2_COLS // NB], BF16, name="c6", align_bytes=64)
             nc.vector.tensor_copy(
                 out=t5[:].rearrange("p (c i j) -> p c j i", i=4, j=PACK),
                 in_=last[:, b * (P // 4):(b + 1) * (P // 4)],
             )
-            quantise(t5, W2_COLS // NB, cq2, "q8", [(("w2half", b), 0)])
+            halves.append(t5)
+        for b in range(NB):
+            quantise(halves[b], W2_COLS // NB, cq2, "q8", [(("w2half", b), 0)])
         for b in range(NB):
             y_ps = psum_y.tile([P, C], F32, name="y_ps%d" % b)
             wc, ws = operand(("w2half", b), 0, P)
@@ -278,11 +281,21 @@ def tile_routed_moe_kernel(tc, xT, w1, w2, gate, offs, pos1, pos2, out):
             else:
                 nc.scalar.copy(out=y_sb[b][:, cols7], in_=y_ps[:])
 
-        for b in range(NB):
-            g1 = wide.tile([P, T], F32, name="g1", tag="wide")
-            g2 = wide.tile([P, T], F32, name="g2", tag="wide")
+        picked = {}
+
+        def pick(b, r, pos_t):
+            got = wide.tile([P, T], F32, name="got", tag="wide")
+            nc.vector.tensor_tensor(got[:], y_sb[b][:].indirect(pos_t[:]), gate_t[:, r, :], MULT)
+            picked[(b, r)] = got
+
+        def finish(b):
             res = wide.tile([P, T], F32, name="res", tag="wide")
-            nc.vector.tensor_tensor(g1[:], y_sb[b][:].indirect(pos1_t[:]), gate_t[:, 0, :], MULT)
-            nc.vector.tensor_tensor(g2[:], y_sb[b][:].indirect(pos2_t[:]), gate_t[:, 1, :], MULT)
-            nc.vector.tensor_tensor(res[:], g1[:], g2[:], ADD)
+            nc.vector.tensor_tensor(res[:], picked[(b, 0)][:], picked[(b, 1)][:], ADD)
             nc.sync.dma_start(out=out[b * P:(b + 1) * P, :], in_=res[:])
+
+        pick(0, 0, pos1_t)
+        pick(0, 1, pos2_t)
+        pick(1, 0, pos1_t)
+        finish(0)
+        pick(1, 1, pos2_t)
+        finish(1)

@@ -42,7 +42,7 @@ def tile_routed_moe_kernel(tc, xT, w1, w2, gate, offs, pos1, pos2, out):
         st3 = ctx.enter_context(tc.tile_pool(name="st3", bufs=3))
         cq2 = ctx.enter_context(tc.tile_pool(name="cq2", bufs=2))
         cq4 = ctx.enter_context(tc.tile_pool(name="cq4", bufs=3))
-        wide = ctx.enter_context(tc.tile_pool(name="wide", bufs=6))
+        wide = ctx.enter_context(tc.tile_pool(name="wide", bufs=8))
         psum_a = ctx.enter_context(tc.psum_pool(name="psum_a", bufs=3))
         psum_y = ctx.enter_context(tc.psum_pool(name="psum_y", bufs=2))
 
@@ -297,5 +297,17 @@ def tile_routed_moe_kernel(tc, xT, w1, w2, gate, offs, pos1, pos2, out):
         pick(0, 1, pos2_t)
         pick(1, 0, pos1_t)
         finish(0)
-        pick(1, 1, pos2_t)
-        finish(1)
+        cuts = (0, 384, T)
+        late = []
+        for k in range(2):
+            lo, hi = cuts[k], cuts[k + 1]
+            got = wide.tile([P, hi - lo], F32, name="got", tag="wide")
+            nc.vector.tensor_tensor(
+                got[:], y_sb[1][:].indirect(pos2_t[:, lo // 16:hi // 16]), gate_t[:, 1, lo:hi], MULT,
+            )
+            late.append(got)
+        for k in range(2):
+            lo, hi = cuts[k], cuts[k + 1]
+            res = wide.tile([P, hi - lo], F32, name="res", tag="wide")
+            nc.vector.tensor_tensor(res[:], picked[(1, 0)][:, lo:hi], late[k][:], ADD)
+            nc.sync.dma_start(out=out[P:2 * P, lo:hi], in_=res[:])

@@ -255,31 +255,32 @@ def tile_routed_moe_kernel(tc, xT, w1, w2, gate, offs, pos1, pos2, out):
         quantise(t1, FULL, cq2, "q6",
                  [(("w2", 4), 0), (("w2", 5), W2_COLS)] + [(("h", e), HALF + (e - 4) * H_COLS) for e in range(4, E)])
         layer2([2, 3, 4, 5], -1)
-        t4 = st2.tile([P, W2_COLS], BF16, name="c5", align_bytes=64)
-        put_w2(t4, 0, 3, 0, "s")
-        quantise(t4, W2_COLS, cq2, "q7", [(("w2", 6), 0)])
-        layer2([6], 0)
-        last = w2_last[7][:].rearrange("p (j c i) -> p c j i", j=PACK, i=4)
-        cols7 = slice(7 * C, 8 * C)
-        halves = []
+        BLOCK_COLS = W2_COLS // NB
+        ends = [st2.tile([P, W2_COLS], BF16, name="c5", align_bytes=64) for b in range(NB)]
+        for e in (6, 7):
+            view = w2_last[e][:].rearrange("p (j c i) -> p c j i", j=PACK, i=4)
+            for b in range(NB):
+                dst = ends[b][:, (e - 6) * BLOCK_COLS:(e - 5) * BLOCK_COLS].rearrange("p (c i j) -> p c j i", i=4, j=PACK)
+                if e == 6:
+                    nc.scalar.copy(out=dst, in_=view[:, b * (P // 4):(b + 1) * (P // 4)])
+                else:
+                    nc.vector.tensor_copy(out=dst, in_=view[:, b * (P // 4):(b + 1) * (P // 4)])
         for b in range(NB):
-            t5 = st2.tile([P, W2_COLS // NB], BF16, name="c6", align_bytes=64)
-            nc.vector.tensor_copy(
-                out=t5[:].rearrange("p (c i j) -> p c j i", i=4, j=PACK),
-                in_=last[:, b * (P // 4):(b + 1) * (P // 4)],
-            )
-            halves.append(t5)
+            quantise(ends[b], W2_COLS, cq2, "q7", [(("w2block", 6, b), 0), (("w2block", 7, b), BLOCK_COLS)])
+        cols67 = slice(6 * C, 8 * C)
         for b in range(NB):
-            quantise(halves[b], W2_COLS // NB, cq2, "q8", [(("w2half", b), 0)])
-        for b in range(NB):
-            y_ps = psum_y.tile([P, C], F32, name="y_ps%d" % b)
-            wc, ws = operand(("w2half", b), 0, P)
-            hc, hs = operand(("h", 7), 0, C)
-            nc.tensor.matmul_mx(out=y_ps[:], lhsT=wc, lhsT_scale=ws, rhs=hc, rhs_scale=hs, start=True, stop=True)
+            y_ps = psum_y.tile([P, 2 * C], F32, name="y_ps%d" % b)
+            for e in (6, 7):
+                wc, ws = operand(("w2block", e, b), 0, P)
+                hc, hs = operand(("h", e), 0, C)
+                nc.tensor.matmul_mx(
+                    out=y_ps[:, (e - 6) * C:(e - 5) * C], lhsT=wc, lhsT_scale=ws, rhs=hc, rhs_scale=hs,
+                    start=True, stop=True,
+                )
             if b == 0:
-                nc.vector.tensor_copy(out=y_sb[b][:, cols7], in_=y_ps[:])
+                nc.vector.tensor_copy(out=y_sb[b][:, cols67], in_=y_ps[:])
             else:
-                nc.scalar.copy(out=y_sb[b][:, cols7], in_=y_ps[:])
+                nc.scalar.copy(out=y_sb[b][:, cols67], in_=y_ps[:])
 
         picked = {}
 
@@ -297,7 +298,7 @@ def tile_routed_moe_kernel(tc, xT, w1, w2, gate, offs, pos1, pos2, out):
         pick(0, 1, pos2_t)
         pick(1, 0, pos1_t)
         finish(0)
-        cuts = (0, 384, T)
+        cuts = (0, 256, T)
         late = []
         for k in range(2):
             lo, hi = cuts[k], cuts[k + 1]

@@ -38,6 +38,8 @@ def tile_routed_moe_kernel(tc, xT, w1, w2, gate, offs, pos1, pos2, out):
         lists = ctx.enter_context(tc.tile_pool(name="lists", bufs=1))
         keep = ctx.enter_context(tc.tile_pool(name="keep", bufs=1))
         raw = ctx.enter_context(tc.tile_pool(name="raw", bufs=4))
+        halves = ctx.enter_context(tc.tile_pool(name="halves", bufs=4))
+        planes = ctx.enter_context(tc.tile_pool(name="planes", bufs=4))
         st2 = ctx.enter_context(tc.tile_pool(name="st2", bufs=2))
         st3 = ctx.enter_context(tc.tile_pool(name="st3", bufs=3))
         cq2 = ctx.enter_context(tc.tile_pool(name="cq2", bufs=2))
@@ -72,12 +74,15 @@ def tile_routed_moe_kernel(tc, xT, w1, w2, gate, offs, pos1, pos2, out):
             nc.sync.dma_start(out=r2[:], in_=w2_view[:, 2 * s:2 * s + 2].rearrange("p e j n -> p e (j n)"))
             w2_raw[s] = r2
 
-        for g in range(PASSES):
-            xr = raw.tile([P, PACK, T], F32, name="raw")
-            nc.sync.dma_start(out=xr[:], in_=x_view[g])
+        for t in range(PACK):
+            xr = planes.tile([P, T], F32, name="plane")
+            nc.sync.dma_start(out=xr[:], in_=x_view[0, :, t, :])
             x_raw.append(xr)
-            if g == 0:
+            if t == 0:
                 nc.sync.dma_start(offs_t[:], offs)
+        xr = raw.tile([P, PACK, T], F32, name="raw")
+        nc.sync.dma_start(out=xr[:], in_=x_view[1])
+        x_raw.append(xr)
         load_w2(0)
         load_w1(0)
         load_w1(1)
@@ -87,23 +92,26 @@ def tile_routed_moe_kernel(tc, xT, w1, w2, gate, offs, pos1, pos2, out):
         nc.sync.dma_start(pos2_t[:], pos2)
         for e in range(4, E):
             load_w1(e)
-        load_w2(1)
-        load_w2(2)
         w2_last = {}
-        for e in (6, 7):
-            r3 = raw.tile([P, W2_COLS], F32, name="raw")
+        for e in (2, 3, 4, 5):
+            r3 = halves.tile([P, W2_COLS], F32, name="half")
             nc.sync.dma_start(out=r3[:], in_=w2_view[:, e].rearrange("p j n -> p (j n)"))
             w2_last[e] = r3
+        w2_block = {}
+        for b in range(NB):
+            for e in (6, 7):
+                r3 = planes.tile([P, PACK, P], F32, name="plane")
+                nc.sync.dma_start(out=r3[:], in_=w2_view[:, e, :, b * P:(b + 1) * P])
+                w2_block[(e, b)] = r3
         gate_t = keep.tile([P, 2, T], F32, name="gate_t")
         nc.sync.dma_start(out=gate_t[:], in_=gate[:, 0:P, :].rearrange("r p t -> p r t"))
 
         y_sb = [keep.tile([P, E * C], F32, name="y_sb%d" % b) for b in range(NB)]
 
-        x_bf = []
-        for g in range(PASSES):
-            xb = keep.tile([P, PACK, T], BF16, name="x_bf%d" % g)
-            nc.vector.tensor_copy(out=xb[:], in_=x_raw[g][:])
-            x_bf.append(xb)
+        x_bf = [keep.tile([P, PACK, T], BF16, name="x_bf%d" % g) for g in range(PASSES)]
+        for t in range(PACK):
+            nc.vector.tensor_copy(out=x_bf[0][:, t, :], in_=x_raw[t][:])
+        nc.vector.tensor_copy(out=x_bf[1][:], in_=x_raw[PACK][:])
 
         where = {}
 
@@ -127,7 +135,7 @@ def tile_routed_moe_kernel(tc, xT, w1, w2, gate, offs, pos1, pos2, out):
 
         def put_w2(stage, off, s, half, engine):
             dst = stage[:, off:off + W2_COLS].rearrange("p (c i j) -> p c j i", i=4, j=PACK)
-            if s < 3:
+            if s == 0:
                 src = w2_raw[s][:, half, :].rearrange("p (j c i) -> p c j i", j=PACK, i=4)
             else:
                 src = w2_last[2 * s + half][:].rearrange("p (j c i) -> p c j i", j=PACK, i=4)
@@ -164,22 +172,19 @@ def tile_routed_moe_kernel(tc, xT, w1, w2, gate, offs, pos1, pos2, out):
                 func=SILU,
             )
 
-        def layer2(experts, vector_block):
-            first = experts[0]
-            cols = slice(first * C, (first + len(experts)) * C)
-            for b in range(NB):
-                y_ps = psum_y.tile([P, len(experts) * C], F32, name="y_ps%d" % b)
-                for i, e in enumerate(experts):
+        def layer2(b, experts):
+            y_ps = psum_y.tile([P, len(experts) * C], F32, name="y_ps%d" % b)
+            for i, e in enumerate(experts):
+                if ("w2", e) in where:
                     wc, ws = operand(("w2", e), b * P, P)
-                    hc, hs = operand(("h", e), 0, C)
-                    nc.tensor.matmul_mx(
-                        out=y_ps[:, i * C:(i + 1) * C], lhsT=wc, lhsT_scale=ws, rhs=hc, rhs_scale=hs,
-                        start=True, stop=True,
-                    )
-                if b == vector_block:
-                    nc.vector.tensor_copy(out=y_sb[b][:, cols], in_=y_ps[:])
                 else:
-                    nc.scalar.copy(out=y_sb[b][:, cols], in_=y_ps[:])
+                    wc, ws = operand(("w2block", e, b), 0, P)
+                hc, hs = operand(("h", e), 0, C)
+                nc.tensor.matmul_mx(
+                    out=y_ps[:, i * C:(i + 1) * C], lhsT=wc, lhsT_scale=ws, rhs=hc, rhs_scale=hs,
+                    start=True, stop=True,
+                )
+            nc.scalar.copy(out=y_sb[b][:, experts[0] * C:(experts[0] + len(experts)) * C], in_=y_ps[:])
 
         stage = {}
 
@@ -244,43 +249,34 @@ def tile_routed_moe_kernel(tc, xT, w1, w2, gate, offs, pos1, pos2, out):
             later_call((3, s), b2, 1)
             layer1(b2, *h_place(b2))
             if s == 2:
-                layer2([0, 1], -1)
+                for b in range(NB):
+                    layer2(b, (0, 1))
 
         t3 = st2.tile([P, HALF], BF16, name="c4", align_bytes=64)
-        put_w2(t3, 0, 1, 0, "v")
+        put_w2(t3, 0, 1, 0, "s")
         put_w2(t3, W2_COLS, 1, 1, "v")
         quantise(t3, HALF, cq2, "q5", [(("w2", 2), 0), (("w2", 3), W2_COLS)])
+        for b in range(NB):
+            layer2(b, (2, 3))
         put_w2(t1, 0, 2, 0, "v")
-        put_w2(t1, W2_COLS, 2, 1, "s")
+        put_w2(t1, W2_COLS, 2, 1, "v")
         quantise(t1, FULL, cq2, "q6",
                  [(("w2", 4), 0), (("w2", 5), W2_COLS)] + [(("h", e), HALF + (e - 4) * H_COLS) for e in range(4, E)])
-        layer2([2, 3, 4, 5], -1)
+        layer2(0, (4, 5))
         BLOCK_COLS = W2_COLS // NB
         ends = [st2.tile([P, W2_COLS], BF16, name="c5", align_bytes=64) for b in range(NB)]
-        for e in (6, 7):
-            view = w2_last[e][:].rearrange("p (j c i) -> p c j i", j=PACK, i=4)
-            for b in range(NB):
+        for b in range(NB):
+            for e in (6, 7):
                 dst = ends[b][:, (e - 6) * BLOCK_COLS:(e - 5) * BLOCK_COLS].rearrange("p (c i j) -> p c j i", i=4, j=PACK)
-                if e == 6:
-                    nc.scalar.copy(out=dst, in_=view[:, b * (P // 4):(b + 1) * (P // 4)])
+                src = w2_block[(e, b)][:].rearrange("p j (c i) -> p c j i", i=4)
+                if b == 0:
+                    nc.scalar.copy(out=dst, in_=src)
                 else:
-                    nc.vector.tensor_copy(out=dst, in_=view[:, b * (P // 4):(b + 1) * (P // 4)])
+                    nc.vector.tensor_copy(out=dst, in_=src)
         for b in range(NB):
             quantise(ends[b], W2_COLS, cq2, "q7", [(("w2block", 6, b), 0), (("w2block", 7, b), BLOCK_COLS)])
-        cols67 = slice(6 * C, 8 * C)
-        for b in range(NB):
-            y_ps = psum_y.tile([P, 2 * C], F32, name="y_ps%d" % b)
-            for e in (6, 7):
-                wc, ws = operand(("w2block", e, b), 0, P)
-                hc, hs = operand(("h", e), 0, C)
-                nc.tensor.matmul_mx(
-                    out=y_ps[:, (e - 6) * C:(e - 5) * C], lhsT=wc, lhsT_scale=ws, rhs=hc, rhs_scale=hs,
-                    start=True, stop=True,
-                )
-            if b == 0:
-                nc.vector.tensor_copy(out=y_sb[b][:, cols67], in_=y_ps[:])
-            else:
-                nc.scalar.copy(out=y_sb[b][:, cols67], in_=y_ps[:])
+        layer2(0, (6, 7))
+        layer2(1, (4, 5, 6, 7))
 
         picked = {}
 

@@ -30,6 +30,7 @@ FULL = 4096
 HALF = 2048
 
 SCALAR_W1 = ((6, 0),)
+VECTOR_GATHERS = (0, 0)
 
 
 def tile_routed_moe_kernel(tc, xT, w1, w2, gate, offs, pos1, pos2, out):
@@ -124,14 +125,14 @@ def tile_routed_moe_kernel(tc, xT, w1, w2, gate, offs, pos1, pos2, out):
                 nc.vector.tensor_copy(out=dst, in_=src)
 
         def put_x(stage, off, e):
+            slots = offs_t[:, e * LIST_COLS:(e + 1) * LIST_COLS]
             for g in range(PASSES):
                 dst = stage[:, off + g * H_COLS:off + (g + 1) * H_COLS].rearrange("p (n t) -> p n t", t=PACK)
                 for t in range(PACK):
-                    nc.scalar.activation(
-                        out=dst[:, :, t],
-                        in_=x_bf[g][:, t, :].indirect(offs_t[:, e * LIST_COLS:(e + 1) * LIST_COLS]),
-                        func=COPY,
-                    )
+                    if (e, g) == VECTOR_GATHERS:
+                        nc.vector.tensor_copy(out=dst[:, :, t], in_=x_raw[t][:].indirect(slots))
+                    else:
+                        nc.scalar.activation(out=dst[:, :, t], in_=x_bf[g][:, t, :].indirect(slots), func=COPY)
 
         def put_w2(stage, off, s, half, engine):
             dst = stage[:, off:off + W2_COLS].rearrange("p (c i j) -> p c j i", i=4, j=PACK)

@@ -1,6 +1,7 @@
 from contextlib import ExitStack
 
 import concourse.mybir as mybir
+from concourse.masks import make_identity
 
 K, T, E, C, H, N = 1024, 512, 8, 128, 512, 256
 FLOPS = 2 * E * C * (K * H + H * N)
@@ -53,6 +54,9 @@ def tile_routed_moe_kernel(tc, xT, w1, w2, gate, offs, pos1, pos2, out):
         warm_out = keep.tile([P, 1], F32, name="warm_out")
         nc.vector.memset(warm_in[:], 0.0)
         nc.scalar.activation(out=warm_out[:], in_=warm_in[:], func=SILU)
+
+        identity = keep.tile([P, P], F32, name="identity")
+        make_identity(nc, identity[:])
 
         offs_t = lists.tile([P, E * C // 16], U16, name="offs_t")
         pos1_t = lists.tile([P, T // 16], U16, name="pos1_t")
@@ -158,7 +162,7 @@ def tile_routed_moe_kernel(tc, xT, w1, w2, gate, offs, pos1, pos2, out):
             return codes[:, cols].bitcast(FP8X4), scales[:, cols]
 
         def layer1(e, h_stage, h_off):
-            a_ps = psum_a.tile([P, PACK, C], F32, name="a_ps")
+            a_ps = psum_a.tile([P, PACK, C], F32, name="a_ps", tag="a_ps")
             for t in range(PACK):
                 for g in range(PASSES):
                     wc, ws = operand(("w1", e, g), t * P, P)
@@ -286,26 +290,27 @@ def tile_routed_moe_kernel(tc, xT, w1, w2, gate, offs, pos1, pos2, out):
             nc.vector.tensor_tensor(got[:], y_sb[b][:].indirect(pos_t[:]), gate_t[:, r, :], MULT)
             picked[(b, r)] = got
 
-        def finish(b):
-            res = wide.tile([P, T], F32, name="res", tag="wide")
-            nc.vector.tensor_tensor(res[:], picked[(b, 0)][:], picked[(b, 1)][:], ADD)
-            nc.sync.dma_start(out=out[b * P:(b + 1) * P, :], in_=res[:])
+        pieces = [(k, slice(k * T // 2, (k + 1) * T // 2)) for k in range(2)]
 
         pick(0, 0, pos1_t)
         pick(0, 1, pos2_t)
+        sums = [psum_a.tile([P, T // 2], F32, name="sum%d" % k, tag="a_ps") for k in range(2)]
+        for r in range(2):
+            for k, cols in pieces:
+                nc.tensor.matmul(sums[k][:], identity[:], picked[(0, r)][:, cols], start=(r == 0), stop=(r == 1))
+        for k, cols in pieces:
+            res = wide.tile([P, T // 2], F32, name="res", tag="wide")
+            nc.scalar.copy(out=res[:], in_=sums[k][:])
+            nc.scalar.dma_start(out=out[0:P, cols], in_=res[:])
         pick(1, 0, pos1_t)
-        finish(0)
-        cuts = (0, 256, T)
         late = []
-        for k in range(2):
-            lo, hi = cuts[k], cuts[k + 1]
-            got = wide.tile([P, hi - lo], F32, name="got", tag="wide")
+        for k, cols in pieces:
+            got = wide.tile([P, T // 2], F32, name="got", tag="wide")
             nc.vector.tensor_tensor(
-                got[:], y_sb[1][:].indirect(pos2_t[:, lo // 16:hi // 16]), gate_t[:, 1, lo:hi], MULT,
+                got[:], y_sb[1][:].indirect(pos2_t[:, cols.start // 16:cols.stop // 16]), gate_t[:, 1, cols], MULT,
             )
             late.append(got)
-        for k in range(2):
-            lo, hi = cuts[k], cuts[k + 1]
-            res = wide.tile([P, hi - lo], F32, name="res", tag="wide")
-            nc.vector.tensor_tensor(res[:], picked[(1, 0)][:, lo:hi], late[k][:], ADD)
-            nc.sync.dma_start(out=out[P:2 * P, lo:hi], in_=res[:])
+        for k, cols in pieces:
+            res = wide.tile([P, T // 2], F32, name="res", tag="wide")
+            nc.vector.tensor_tensor(res[:], picked[(1, 0)][:, cols], late[k][:], ADD)
+            nc.sync.dma_start(out=out[P:2 * P, cols], in_=res[:])

@@ -294,15 +294,17 @@ def tile_routed_moe_kernel(tc, xT, w1, w2, gate, offs, pos1, pos2, out):
 
         pick(0, 0, pos1_t)
         pick(0, 1, pos2_t)
-        sums = [psum_a.tile([P, T // 2], F32, name="sum%d" % k, tag="a_ps") for k in range(2)]
+        first, second = pieces[0][1], pieces[1][1]
+        total = psum_a.tile([P, T // 2], F32, name="total", tag="a_ps")
         for r in range(2):
-            for k, cols in pieces:
-                nc.tensor.matmul(sums[k][:], identity[:], picked[(0, r)][:, cols], start=(r == 0), stop=(r == 1))
-        for k, cols in pieces:
-            res = wide.tile([P, T // 2], F32, name="res", tag="wide")
-            nc.scalar.copy(out=res[:], in_=sums[k][:])
-            nc.scalar.dma_start(out=out[0:P, cols], in_=res[:])
+            nc.tensor.matmul(total[:], identity[:], picked[(0, r)][:, first], start=(r == 0), stop=(r == 1))
+        res = wide.tile([P, T // 2], F32, name="res", tag="wide")
+        nc.scalar.copy(out=res[:], in_=total[:])
+        nc.sync.dma_start(out=out[0:P, first], in_=res[:])
         pick(1, 0, pos1_t)
+        res = wide.tile([P, T // 2], F32, name="res", tag="wide")
+        nc.vector.tensor_tensor(res[:], picked[(0, 0)][:, second], picked[(0, 1)][:, second], ADD)
+        nc.sync.dma_start(out=out[0:P, second], in_=res[:])
         late = []
         for k, cols in pieces:
             got = wide.tile([P, T // 2], F32, name="got", tag="wide")

from contextlib import ExitStack

import concourse.mybir as mybir
from concourse.masks import make_identity

K, T, E, C, H, N = 1024, 512, 8, 128, 512, 256
FLOPS = 2 * E * C * (K * H + H * N)

F32 = mybir.dt.float32
BF16 = mybir.dt.bfloat16
U32 = mybir.dt.uint32
U16 = mybir.dt.uint16
U8 = mybir.dt.uint8
FP8X4 = mybir.dt.float8_e4m3fn_x4
MULT = mybir.AluOpType.mult
ADD = mybir.AluOpType.add
SILU = mybir.ActivationFunctionType.Silu
COPY = mybir.ActivationFunctionType.Copy

P = 128
PACK = 4
PASSES = 2
LIST_COLS = C // 16
NB = N // P
PAIRS = E // 2
W1_COLS = H * PACK
X_COLS = PASSES * C * PACK
W2_COLS = N * PACK
H_COLS = C * PACK
FULL = 4096
HALF = 2048

SCALAR_W1 = ((6, 0),)
VECTOR_GATHERS = (0, 0)


def tile_routed_moe_kernel(tc, xT, w1, w2, gate, offs, pos1, pos2, out):
    nc = tc.nc
    with ExitStack() as ctx:
        lists = ctx.enter_context(tc.tile_pool(name="lists", bufs=1))
        keep = ctx.enter_context(tc.tile_pool(name="keep", bufs=1))
        raw = ctx.enter_context(tc.tile_pool(name="raw", bufs=4))
        halves = ctx.enter_context(tc.tile_pool(name="halves", bufs=4))
        planes = ctx.enter_context(tc.tile_pool(name="planes", bufs=4))
        st2 = ctx.enter_context(tc.tile_pool(name="st2", bufs=2))
        st3 = ctx.enter_context(tc.tile_pool(name="st3", bufs=3))
        cq2 = ctx.enter_context(tc.tile_pool(name="cq2", bufs=2))
        cq4 = ctx.enter_context(tc.tile_pool(name="cq4", bufs=3))
        wide = ctx.enter_context(tc.tile_pool(name="wide", bufs=8))
        psum_a = ctx.enter_context(tc.psum_pool(name="psum_a", bufs=3))
        psum_y = ctx.enter_context(tc.psum_pool(name="psum_y", bufs=2))

        warm_in = keep.tile([P, 1], F32, name="warm_in")
        warm_out = keep.tile([P, 1], F32, name="warm_out")
        nc.vector.memset(warm_in[:], 0.0)
        nc.scalar.activation(out=warm_out[:], in_=warm_in[:], func=SILU)

        identity = keep.tile([P, P], F32, name="identity")
        make_identity(nc, identity[:])

        offs_t = lists.tile([P, E * C // 16], U16, name="offs_t")
        pos1_t = lists.tile([P, T // 16], U16, name="pos1_t")
        pos2_t = lists.tile([P, T // 16], U16, name="pos2_t")
        x_view = xT.rearrange("(g p t) n -> g p t n", p=P, t=PACK)
        w1_view = w1.rearrange("e (g p j) c -> e g p j c", p=P, j=PACK)
        w2_view = w2.rearrange("e (p j) n -> p e j n", j=PACK)
        x_raw = []
        w1_raw = {}
        w2_raw = {}

        def load_w1(e):
            for g in range(PASSES):
                r1 = raw.tile([P, PACK, H], F32, name="raw")
                nc.sync.dma_start(out=r1[:], in_=w1_view[e, g])
                w1_raw[(e, g)] = r1

        def load_w2(s):
            r2 = raw.tile([P, 2, W2_COLS], F32, name="raw")
            nc.sync.dma_start(out=r2[:], in_=w2_view[:, 2 * s:2 * s + 2].rearrange("p e j n -> p e (j n)"))
            w2_raw[s] = r2

        for t in range(PACK):
            xr = planes.tile([P, T], F32, name="plane")
            nc.sync.dma_start(out=xr[:], in_=x_view[0, :, t, :])
            x_raw.append(xr)
            if t == 0:
                nc.sync.dma_start(offs_t[:], offs)
        xr = raw.tile([P, PACK, T], F32, name="raw")
        nc.sync.dma_start(out=xr[:], in_=x_view[1])
        x_raw.append(xr)
        load_w2(0)
        load_w1(0)
        load_w1(1)
        load_w1(2)
        load_w1(3)
        nc.sync.dma_start(pos1_t[:], pos1)
        nc.sync.dma_start(pos2_t[:], pos2)
        for e in range(4, E):
            load_w1(e)
        w2_last = {}
        for e in (2, 3, 4, 5):
            r3 = halves.tile([P, W2_COLS], F32, name="half")
            nc.sync.dma_start(out=r3[:], in_=w2_view[:, e].rearrange("p j n -> p (j n)"))
            w2_last[e] = r3
        w2_block = {}
        for b in range(NB):
            for e in (6, 7):
                r3 = planes.tile([P, PACK, P], F32, name="plane")
                nc.sync.dma_start(out=r3[:], in_=w2_view[:, e, :, b * P:(b + 1) * P])
                w2_block[(e, b)] = r3
        gate_t = keep.tile([P, 2, T], F32, name="gate_t")
        nc.sync.dma_start(out=gate_t[:], in_=gate[:, 0:P, :].rearrange("r p t -> p r t"))

        y_sb = [keep.tile([P, E * C], F32, name="y_sb%d" % b) for b in range(NB)]

        x_bf = [keep.tile([P, PACK, T], BF16, name="x_bf%d" % g) for g in range(PASSES)]
        for t in range(PACK):
            nc.vector.tensor_copy(out=x_bf[0][:, t, :], in_=x_raw[t][:])
        nc.vector.tensor_copy(out=x_bf[1][:], in_=x_raw[PACK][:])

        where = {}

        def put_w1(stage, off, e, g):
            src = w1_raw[(e, g)][:].rearrange("p j (m t) -> p m j t", t=PACK)
            dst = stage[:, off:off + W1_COLS].rearrange("p (t m j) -> p m j t", t=PACK, j=PACK)
            if (e, g) in SCALAR_W1:
                nc.scalar.copy(out=dst, in_=src)
            else:
                nc.vector.tensor_copy(out=dst, in_=src)

        def put_x(stage, off, e):
            slots = offs_t[:, e * LIST_COLS:(e + 1) * LIST_COLS]
            for g in range(PASSES):
                dst = stage[:, off + g * H_COLS:off + (g + 1) * H_COLS].rearrange("p (n t) -> p n t", t=PACK)
                for t in range(PACK):
                    if (e, g) == VECTOR_GATHERS:
                        nc.vector.tensor_copy(out=dst[:, :, t], in_=x_raw[t][:].indirect(slots))
                    else:
                        nc.scalar.activation(out=dst[:, :, t], in_=x_bf[g][:, t, :].indirect(slots), func=COPY)

        def put_w2(stage, off, s, half, engine):
            dst = stage[:, off:off + W2_COLS].rearrange("p (c i j) -> p c j i", i=4, j=PACK)
            if s == 0:
                src = w2_raw[s][:, half, :].rearrange("p (j c i) -> p c j i", j=PACK, i=4)
            else:
                src = w2_last[2 * s + half][:].rearrange("p (j c i) -> p c j i", j=PACK, i=4)
            if engine == "s":
                nc.scalar.copy(out=dst, in_=src)
            else:
                nc.vector.tensor_copy(out=dst, in_=src)

        def quantise(stage, width, pool, tag, parts):
            codes = pool.tile([P, width // PACK], U32, name=tag + "c", align_bytes=64)
            scales = pool.tile([P, width // PACK], U8, name=tag + "s", align_bytes=64)
            nc.vector.quantize_mx(out=codes[:].bitcast(FP8X4), scales=scales[:], in_=stage[:])
            for key, off in parts:
                where[key] = (codes, scales, off // PACK)

        def operand(key, first, count):
            codes, scales, base = where[key]
            cols = slice(base + first, base + first + count)
            return codes[:, cols].bitcast(FP8X4), scales[:, cols]

        def layer1(e, h_stage, h_off):
            a_ps = psum_a.tile([P, PACK, C], F32, name="a_ps", tag="a_ps")
            for t in range(PACK):
                for g in range(PASSES):
                    wc, ws = operand(("w1", e, g), t * P, P)
                    xc, xs = operand(("x", e), g * C, C)
                    nc.tensor.matmul_mx(
                        out=a_ps[:, t, :], lhsT=wc, lhsT_scale=ws, rhs=xc, rhs_scale=xs,
                        start=(g == 0), stop=(g == PASSES - 1),
                    )
            nc.scalar.activation(
                out=h_stage[:, h_off:h_off + H_COLS].rearrange("p (n t) -> p n t", t=PACK),
                in_=a_ps[:].rearrange("p t n -> p n t"),
                func=SILU,
            )

        def layer2(b, experts):
            y_ps = psum_y.tile([P, len(experts) * C], F32, name="y_ps%d" % b)
            for i, e in enumerate(experts):
                if ("w2", e) in where:
                    wc, ws = operand(("w2", e), b * P, P)
                else:
                    wc, ws = operand(("w2block", e, b), 0, P)
                hc, hs = operand(("h", e), 0, C)
                nc.tensor.matmul_mx(
                    out=y_ps[:, i * C:(i + 1) * C], lhsT=wc, lhsT_scale=ws, rhs=hc, rhs_scale=hs,
                    start=True, stop=True,
                )
            nc.scalar.copy(out=y_sb[b][:, experts[0] * C:(experts[0] + len(experts)) * C], in_=y_ps[:])

        stage = {}

        def x_parts(pair):
            return [(("x", 2 * pair), W1_COLS), (("x", 2 * pair + 1), W1_COLS + X_COLS)]

        def tokens(pair, key):
            if key[0] == 2:
                stage[key] = st2.tile([P, FULL], BF16, name="c2", align_bytes=64)
            else:
                stage[key] = st3.tile([P, FULL], BF16, name="c3", align_bytes=64)
            put_x(stage[key], W1_COLS, 2 * pair)
            put_x(stage[key], W1_COLS + X_COLS, 2 * pair + 1)

        tokens(0, (2, 0))
        stage[(3, 0)] = st3.tile([P, FULL], BF16, name="c3", align_bytes=64)
        put_w2(stage[(3, 0)], W1_COLS, 0, 0, "v")
        put_w2(stage[(3, 0)], W1_COLS + W2_COLS, 0, 1, "v")
        tokens(1, (2, 1))
        tokens(2, (3, 1))
        stage[(3, 2)] = st3.tile([P, FULL], BF16, name="c3", align_bytes=64)
        t1 = keep.tile([P, FULL], BF16, name="t1", align_bytes=64)
        extra = {
            (2, 0): x_parts(0),
            (2, 1): x_parts(1),
            (3, 1): x_parts(2),
            (2, 2): x_parts(3),
            (3, 0): [(("w2", 0), W1_COLS), (("w2", 1), W1_COLS + W2_COLS)],
            (3, 2): [(("h", e), W1_COLS + e * H_COLS) for e in range(4)],
        }

        def h_place(e):
            if e < 4:
                return stage[(3, 2)], W1_COLS + e * H_COLS
            return t1, HALF + (e - 4) * H_COLS

        def later_call(key, e, g):
            if key in extra:
                put_w1(stage[key], 0, e, g)
                if key[0] == 2:
                    quantise(stage[key], FULL, cq2, "q2", [(("w1", e, g), 0)] + extra[key])
                else:
                    quantise(stage[key], FULL, cq4, "q3", [(("w1", e, g), 0)] + extra[key])
            else:
                c4 = st2.tile([P, HALF], BF16, name="c4", align_bytes=64)
                put_w1(c4, 0, e, g)
                quantise(c4, HALF, cq4, "q4", [(("w1", e, g), 0)])

        for s in range(PAIRS):
            a, b2 = 2 * s, 2 * s + 1
            c1 = st2.tile([P, FULL], BF16, name="c1", align_bytes=64)
            put_w1(c1, 0, a, 0)
            put_w1(c1, W1_COLS, a, 1)
            quantise(c1, FULL, cq2, "q1", [(("w1", a, 0), 0), (("w1", a, 1), W1_COLS)])
            if s >= 2:
                layer1(a, *h_place(a))
            later_call((2, s), b2, 0)
            if s < 2:
                layer1(a, *h_place(a))
            if s == 0:
                tokens(3, (2, 2))
            later_call((3, s), b2, 1)
            layer1(b2, *h_place(b2))
            if s == 2:
                for b in range(NB):
                    layer2(b, (0, 1))

        t3 = st2.tile([P, HALF], BF16, name="c4", align_bytes=64)
        put_w2(t3, 0, 1, 0, "s")
        put_w2(t3, W2_COLS, 1, 1, "v")
        quantise(t3, HALF, cq2, "q5", [(("w2", 2), 0), (("w2", 3), W2_COLS)])
        for b in range(NB):
            layer2(b, (2, 3))
        put_w2(t1, 0, 2, 0, "v")
        put_w2(t1, W2_COLS, 2, 1, "v")
        quantise(t1, FULL, cq2, "q6",
                 [(("w2", 4), 0), (("w2", 5), W2_COLS)] + [(("h", e), HALF + (e - 4) * H_COLS) for e in range(4, E)])
        layer2(0, (4, 5))
        BLOCK_COLS = W2_COLS // NB
        ends = [st2.tile([P, W2_COLS], BF16, name="c5", align_bytes=64) for b in range(NB)]
        for b in range(NB):
            for e in (6, 7):
                dst = ends[b][:, (e - 6) * BLOCK_COLS:(e - 5) * BLOCK_COLS].rearrange("p (c i j) -> p c j i", i=4, j=PACK)
                src = w2_block[(e, b)][:].rearrange("p j (c i) -> p c j i", i=4)
                if b == 0:
                    nc.scalar.copy(out=dst, in_=src)
                else:
                    nc.vector.tensor_copy(out=dst, in_=src)
        for b in range(NB):
            quantise(ends[b], W2_COLS, cq2, "q7", [(("w2block", 6, b), 0), (("w2block", 7, b), BLOCK_COLS)])
        layer2(0, (6, 7))
        layer2(1, (4, 5, 6, 7))

        picked = {}

        def pick(b, r, pos_t):
            got = wide.tile([P, T], F32, name="got", tag="wide")
            nc.vector.tensor_tensor(got[:], y_sb[b][:].indirect(pos_t[:]), gate_t[:, r, :], MULT)
            picked[(b, r)] = got

        pieces = [(k, slice(k * T // 2, (k + 1) * T // 2)) for k in range(2)]

        pick(0, 0, pos1_t)
        pick(0, 1, pos2_t)
        first, second = pieces[0][1], pieces[1][1]
        total = psum_a.tile([P, T // 2], F32, name="total", tag="a_ps")
        for r in range(2):
            nc.tensor.matmul(total[:], identity[:], picked[(0, r)][:, first], start=(r == 0), stop=(r == 1))
        res = wide.tile([P, T // 2], F32, name="res", tag="wide")
        nc.scalar.copy(out=res[:], in_=total[:])
        nc.sync.dma_start(out=out[0:P, first], in_=res[:])
        pick(1, 0, pos1_t)
        res = wide.tile([P, T // 2], F32, name="res", tag="wide")
        nc.vector.tensor_tensor(res[:], picked[(0, 0)][:, second], picked[(0, 1)][:, second], ADD)
        nc.sync.dma_start(out=out[0:P, second], in_=res[:])
        late = []
        for k, cols in pieces:
            got = wide.tile([P, T // 2], F32, name="got", tag="wide")
            nc.vector.tensor_tensor(
                got[:], y_sb[1][:].indirect(pos2_t[:, cols.start // 16:cols.stop // 16]), gate_t[:, 1, cols], MULT,
            )
            late.append(got)
        for k, cols in pieces:
            res = wide.tile([P, T // 2], F32, name="res", tag="wide")
            nc.vector.tensor_tensor(res[:], picked[(1, 0)][:, cols], late[k][:], ADD)
            nc.sync.dma_start(out=out[P:2 * P, cols], in_=res[:])
